import numpy as np, ml_dtypes
CORES = [40,41,42,43,44,45,46,47]
N = 8
import mx_ref
BF = ml_dtypes.bfloat16
def gentries(a):
    return np.ascontiguousarray(a.reshape(8, 16, -1).transpose(0, 2, 1)).reshape(8, -1)
def gtable(e):
    e = np.asarray(e); return np.ascontiguousarray(e.reshape(8, -1, 16).transpose(0, 2, 1)).reshape(128, -1).astype(np.int32)
def gcols(t, e):
    v = np.concatenate([t.reshape(8, 16, -1, 4), np.zeros((8, 16, 1, 4), BF)], axis=2)
    return np.ascontiguousarray(np.stack([v[g][:, e[g]] for g in range(8)])).reshape(128, -1)
def gpick(z, e):
    return np.concatenate([z[16 * g:16 * g + 16][:, e[g]] for g in range(8)])
def tile(rs):
    return np.stack(rs, axis=2).reshape(128, -1).astype(BF)
def pick(q, e):
    c = np.concatenate([q[0].reshape(128, -1, 4), np.zeros((128, 1, 4), np.uint8)], axis=1); s = np.concatenate([q[1], np.ones((16, 1), np.uint8)], axis=1)
    return (np.ascontiguousarray(c[:, e].reshape(128, -1)), np.ascontiguousarray(s[:, e]))
def join(*qs):
    return (np.concatenate([q[0] for q in qs], axis=1), np.concatenate([q[1] for q in qs], axis=1))
def put(q, e, v):
    c, s = q[0].reshape(128, -1, 4).copy(), q[1].copy(); c[:, e] = v[0].reshape(128, -1, 4); s[:, e] = v[1]
    return (c.reshape(128, -1), s)
def pk(c, s):
    return (np.ascontiguousarray(c), mx_ref.live(s))
def emit(q):
    return q[0], q[1]
def packed(v, rng):
    q = [mx_ref.quantize(np.ascontiguousarray(v[r])) for r in range(N)]
    return np.stack([a for a, b in q]), np.stack([mx_ref.plane(b, rng) for a, b in q])
def values_of_codes():
    e, c = np.zeros((128, 128, 4), np.float32), np.zeros((128, 2, 4), np.uint8)
    e[np.arange(128), np.arange(128), 0] = 1
    c[:127, :, 0] = np.arange(256).reshape(2, 128).T[:127]
    return mx_ref.matmul(mx_ref.quantize(e.reshape(128, 512).astype(BF)), (c.reshape(128, 8), np.full((16, 2), 127, np.uint8))).T.reshape(-1).astype(np.float64)
CODE_VALUE, SCALE_VALUE = values_of_codes(), 2.0 ** (np.arange(256) - 127.0)
def decode(q):
    return (CODE_VALUE[q[0]].reshape(16, 8, -1, 4) * SCALE_VALUE[q[1]][:, None, :, None] + 0.0).reshape(128, -1).astype(np.float32)
def f(rng, *shape):
    return mx_ref.flush((rng.standard_normal(shape, dtype=np.float32) * np.exp2(rng.integers(-2, 3, shape[:-1] + (1,)))).astype(BF))
def wide(rng, *shape, cols=0):
    v = rng.standard_normal(shape, dtype=np.float32) * np.exp2(rng.integers(-12, 13, shape)).astype(np.float32)
    if cols: v *= np.repeat(np.exp2(rng.integers(-cols, cols + 1, shape[:-2] + (1, shape[-1] // 4))) * (rng.random(shape[:-2] + (1, shape[-1] // 4)) > 0.0625), 4, axis=-1).astype(np.float32)
    return mx_ref.flush(v.astype(BF))
C, B = 320, 160
STEP = [1, 2, 4]
def big(v):
    v = v.astype(np.float32)
    v[np.abs(v) < np.float32(2.0 ** -16)] = 0
    return v.astype(BF)
def numbers_of(rng):
    return {"x": big(f(rng, N, 128, 4 * C)), "u": np.array(f(rng, N, 128, 512)), "v": np.array(f(rng, N, 128, 512))}
def layers(rng):
    k = np.stack([np.exp2(rng.permutation(128) % 5 - 2.0) for r in range(N)])[:, :, None].astype(np.float32)
    return big(rng.standard_normal((N, 128, 2048), dtype=np.float32) * k).reshape(N, 8, 16, 4, 8, 16, 4)
def weights(rng, w):
    c, p = packed(np.ascontiguousarray(w).reshape(N, 128, 2048), rng)
    return {"wc": c, "ws": p}
def still(w, parts):
    for i in parts:
        w[:, :, i] = 0
        w[:, :, :, :, :, i] = 0
    return w
def lists(rng, how, label):
    o, m = np.zeros((N, 8, C), int), np.zeros((N, 8, C), int)
    i = np.arange(B)
    for r in range(N):
        for g in range(8):
            e = rng.permutation(C)
            s, t = [(e[:B], e[B:]), (i, C - 1 - i), (i, B + i), (2 * i, 2 * i + 1), (2 * i + 1, (2 * i + 2) % C), (B + i, B - 1 - i)][how[r, g]]
            j, k = [(rng.permutation(B), rng.permutation(B)), (i, i), (B - 1 - i, B - 1 - i)][label[r, g]]
            o[r, g, s] = j
            o[r, g, t] = B + k
            m[r, g, j] = B + k
            m[r, g, B + k] = j
    return {"o": np.stack([gtable(o[r]) for r in range(N)]), "m": np.stack([gtable(m[r]) for r in range(N)])}
NONE = np.zeros((N, 8), int)
def setup_inputs(rng):
    return {**numbers_of(rng), **lists(rng, NONE, NONE), **weights(rng, layers(rng))}
def setup_inputs_ties(rng):
    d = numbers_of(rng)
    x = d["x"].reshape(N, 8, 16, C, 4)
    x[:, :, 0] = 0
    x[:, :, 0, :, 0] = rng.integers(0, 3, (N, 8, C)).astype(np.float32).astype(BF)
    u = d["u"].reshape(N, 128, 128, 4)
    u[:, :, ::16] = 0
    z = rng.permutation(N)
    for r in range(N):
        for h in range(0, 128, 16): u[r, h, h, 0] = 0.0 if z[r] == 0 else -1.0 if z[r] == 1 else 1.0
    how = (rng.permutation(N)[:, None] + np.arange(8)) % 6
    return {"x": x.reshape(N, 128, 4 * C), "u": u.reshape(N, 128, 512), "v": d["v"], **lists(rng, how, NONE), **weights(rng, still(layers(rng), [0]))}
def setup_inputs_near(rng):
    d = numbers_of(rng)
    x = d["x"].astype(np.float32).reshape(N, 8, 16, C, 4)
    x[:, :, 0] = 0
    x[:, :, 8:] = 0
    u = d["u"].reshape(N, 128, 128, 4)
    u[:, :, ::16] = 0
    z = rng.permutation(N) % 4
    for r in range(N):
        s = rng.integers(0, 16, (8, C))
        c = rng.integers(0, 2, (8, C)) * 2.0 - 1.0
        k = 1.0 if z[r] == 0 else 2.0 ** -30
        if z[r] < 3:
            x[r, :, 0, :, 0] = c if z[r] < 2 else c * (rng.random((8, C)) < 0.25)
            x[r, :, 8] = ((s[:, :, None] >> np.arange(4)) & 1) * np.exp2(np.arange(4) - 23.0)
        else:
            x[r, :, 10, :, 0] = (s % 2) * 1.125 * 2.0 ** -29
            x[r, :, 12, :, 0] = (1 - s % 2) * 2.0 ** -29
        if z[r] < 2: x[r, :, 11, :, 0] = 2.0 ** -10
        for h in range(0, 128, 16):
            if z[r] < 3:
                u[r, h, h, 0] = 1.0 if z[r] == 2 else k
                u[r, h + 8, h] = k
                u[r, h + 11, h, 0] = k
            else:
                u[r, h + 10, h, 0] = 1.125 * k
                u[r, h + 12, h, 0] = 1.25 * k
    return {"x": x.reshape(N, 128, 4 * C).astype(BF), "u": u.reshape(N, 128, 512), "v": d["v"], **lists(rng, NONE, NONE), **weights(rng, still(layers(rng), [0, 8, 9, 10, 11, 12, 13, 14, 15]))}
def setup_inputs_fine(rng):
    d = numbers_of(rng)
    e = rng.integers(8, 15, (N, 8, 16, C, 4))
    e[:, :, 1] = (8 + (np.arange(N)[:, None] + np.arange(8)) % 7)[:, :, None, None]
    x = (1.125 + 0.25 * rng.integers(0, 4, (N, 8, 16, C, 4))) * np.exp2(-e.astype(np.float64))
    x[:, :, ::8, :, 0] = 1.96875
    x *= rng.integers(0, 2, x.shape) * 2.0 - 1.0
    x *= np.exp2(rng.integers(-2, 3, (N, 1, 1, C, 1)).astype(np.float64))
    u = d["u"].reshape(N, 128, 128, 4)
    u[:, :, ::16] = 0
    for h in range(0, 128, 16): u[:, h + 1, h] = 1.0
    w = layers(rng)
    w[:, :, ::8, :, :, :, 0] = 0
    return {"x": x.astype(np.float32).reshape(N, 128, 4 * C).astype(BF), "u": u.reshape(N, 128, 512), "v": d["v"], **lists(rng, NONE, NONE), **weights(rng, w)}
def setup_inputs_ends(rng):
    d = numbers_of(rng)
    z = rng.permutation(N) % 4
    how = np.stack([rng.permutation(np.array([0, 1, 2, 2, 2, 3, 4, 5])) for r in range(N)])
    l = lists(rng, how, np.repeat(1 + z[:, None] % 2, 8, axis=1))
    x = d["x"].reshape(N, 8, 16, C, 4)
    u = d["u"].reshape(N, 128, 128, 4)
    v = d["v"]
    w = layers(rng).reshape(N, 128, 2048)
    for r in range(N):
        c = (1.0 - 2.0 * (np.argsort(gentries(l["o"][r]), axis=1) % 2)) * [2.0 ** 19, -2.0 ** -29, 0.0, 0.0][z[r]]
        if z[r] < 2:
            u[r, :, ::16] = 0
            for h in range(0, 128, 16): u[r, h:h + 16, h] = [2.0 ** 30, 2.0 ** -30][z[r]]
        else:
            k = 5.0 - 2.0 * z[r]
            c = np.full((8, C), k * 2.0 ** 19)
            u[r, :, ::16] = k * 2.0 ** 30
            v[r] = k * 2.0 ** 30
            w[r] = 2.0
        if z[r] == 1: w[r] = 0
        x[r] = c[:, None, :, None].astype(np.float32).astype(BF)
    v = (np.where(v < 0, -1.0, 1.0) * np.where(rng.permutation(N) % 2, 2.0 ** -30, 2.0 ** 30)[:, None, None]).astype(np.float32).astype(BF)
    return {"x": x.reshape(N, 128, 4 * C), "u": u.reshape(N, 128, 512), "v": v, **l, **weights(rng, w)}
def setup_inputs_spread(rng):
    d = setup_inputs(rng)
    d["x"] = big(wide(rng, N, 128, 4 * C, cols=4))
    return d
def check_inputs(d):
    b = []
    for k, lo, hi in (("x", 2.0 ** -29, 2.0 ** 19), ("u", 2.0 ** -30, 2.0 ** 30), ("v", 2.0 ** -30, 2.0 ** 30)):
        a = np.abs(d[k].astype(np.float32))
        if not (np.isfinite(a).all() and ((a == 0) | (a >= lo) & (a <= hi)).all()): b.append("a value of " + k)
    none, least, most = [emit(mx_ref.quantize(np.full((128, 16), k, np.float32).astype(BF)))[1][0, 0] for k in (0.0, 2.0 ** -30, 2.0 ** 30)]
    i = np.arange(C)
    for r in range(N):
        o, m = gentries(d["o"][r]), gentries(d["m"][r])
        if (np.sort(o, axis=1) != i).any(): b.append("o: not every item once")
        if (np.sort(m, axis=1) != i).any() or (np.take_along_axis(m, m, axis=1) != i).any() or (m[:, :B] < B).any(): b.append("m: not mates of births and deaths")
        if ((d["wc"][r] == 0x7F) | (d["wc"][r] == 0xFF)).any(): b.append("wc: a code that is no number")
        s = mx_ref.live(d["ws"][r])
        if ((s != none) & ((s < least) | (s > most))).any(): b.append("ws: a scale out of range")
        elif not (np.sum(np.abs(decode(pk(d["wc"][r], d["ws"][r])).astype(np.float64)).reshape(128, 512, 4), axis=(0, 2)) <= 1024).all(): b.append("W: a column's sum of sizes")
    return b
def of(a, i):
    return np.take_along_axis(a, i, axis=2)
def reference(x, u, v, o, m, wc, ws):
    qu = [mx_ref.quantize(u[r]) for r in range(N)]
    lay = [pk(wc[r], ws[r]) for r in range(N)]
    now = [x[r] for r in range(N)]
    at = np.stack([gentries(o[r]) for r in range(N)])
    mate = np.stack([gentries(m[r]) for r in range(N)])
    for t in range(3):
        k = t % 2
        q = [mx_ref.quantize(now[r]) for r in range(N)]
        held = [decode(q[r]).astype(BF) for r in range(N)]
        s = np.stack([mx_ref.matmul(qu[r], q[r])[::16] for r in range(N)]) + np.float32(0.0)
        place = np.argsort(at, axis=2)
        lo, hi = np.minimum(place, of(place, mate)), np.maximum(place, of(place, mate))
        a, b = at[:, :, k:C - 1:2].copy(), at[:, :, k + 1::2].copy()
        turn = (of(s, a) > of(s, b)) & (of(mate, a) != b)
        nest = (of(lo, a) < of(lo, b)) & (of(hi, b) < of(hi, a)) | (of(lo, b) < of(lo, a)) & (of(hi, a) < of(hi, b))
        switch = turn & nest & ((a < B) == (b < B))
        at2 = at.copy()
        at2[:, :, k:C - 1:2] = np.where(turn, b, a)
        at2[:, :, k + 1::2] = np.where(turn, a, b)
        c = np.zeros((N, 8, C), np.int64) + np.arange(C)
        np.put_along_axis(c, a, np.where(switch, b, a), axis=2)
        np.put_along_axis(c, b, np.where(switch, a, b), axis=2)
        mate2 = of(c, of(mate, c))
        place2 = np.argsort(at2, axis=2)
        gives = of(mate2, at2)[:, :, :B]
        sent = [mx_ref.quantize(gcols(held[r], gives[r])) for r in range(N)]
        met = np.where(place2 < B, place2, B + mate2)
        for r in range(N):
            own = gcols(held[r], mate[r])
            both = np.concatenate([decode(sent[r ^ STEP[t]]).astype(BF), held[r]], axis=1)
            z = mx_ref.quantize(((own.astype(np.float32) + gcols(both, met[r]).astype(np.float32)) * np.float32(0.5)).astype(BF))
            now[r] = tile([gpick(mx_ref.matmul(pick(lay[r], np.arange(128 * i, 128 * i + 128)), z) * np.float32(0.0078125), mate2[r]) + own[:, i::4].astype(np.float32) for i in range(4)])
        at, mate = at2, mate2
    y, om = np.zeros((N, 128, C), np.float32), np.zeros((N, 8, 2 * C), np.float32)
    oc, osc = np.zeros((N, 128, 4 * C), np.uint8), np.zeros((N, 16, C), np.uint8)
    for r in range(N):
        q = mx_ref.quantize(now[r])
        y[r] = mx_ref.matmul(mx_ref.quantize(v[r]), q)
        om[r] = np.concatenate([at[r], mate[r]], axis=1)
        oc[r], osc[r] = emit(q)
    return {"y": y, "om": om, "oc": oc, "osc": osc}

@@ -1,0 +1,475 @@
+from concourse.mybir import dt, AluOpType as OP, ActivationFunctionType as AF
+
+C, B = 320, 160
+STEP = [1, 2, 4]
+EW = 176
+WD = C + EW
+NE = [160, 162, 160]
+F8, BF, F32, U16, U8, I32 = "float8_e4m3fn_x4", "bfloat16", "float32", "uint16", "uint8", "int32"
+LW = 640
+PB = 839
+
+SCRATCH = {
+    "oi": ("sbuf", [128, 20], I32), "mi": ("sbuf", [128, 20], I32),
+    "x0": ("sbuf", [128, 4 * C], BF), "ut": ("sbuf", [128, 512], BF), "vt": ("sbuf", [128, 512], BF),
+    "wq": ("sbuf", [128, 512], F8), "wp": ("sbuf", [128, 512], U8),
+    "uq": ("sbuf", [128, 128], F8), "up": ("sbuf", [128, 128], U8),
+    "uq16": ("sbuf", [128, 128], F8), "up16": ("sbuf", [128, 128], U8),
+    "vq": ("sbuf", [128, 128], F8), "vp": ("sbuf", [128, 128], U8),
+    "ect": ("sbuf", [128, 516], BF), "ones": ("sbuf", [128, 516], BF),
+    "eq": ("sbuf", [128, 512], F8), "ep": ("sbuf", [128, 512], U8),
+    "iota": ("sbuf", [128, C], BF), "cw": ("sbuf", [128, C], BF), "bw": ("sbuf", [128, 8], F32),
+    "j16": ("sbuf", [128, C], BF), "mask": ("sbuf", [128, LW], BF), "hold": ("sbuf", [128, LW], BF),
+    "pcol": ("sbuf", [128, 8], I32), "pcol2": ("sbuf", [128, 8], I32), "uli": ("sbuf", [128, 8], I32), "ulu": ("sbuf", [128, 8], U16),
+    "kpat": ("sbuf", [128, 20], F32),
+    "tb": ("sbuf", [128, 3000], F32), "ub": ("sbuf", [128, 1000], U16),
+    "mrow": ("sbuf", [128, C], BF), "orow": ("sbuf", [128, C], BF), "prow": ("sbuf", [128, C], BF),
+    "wf": ("sbuf", [128, 4 * WD], BF),
+    "ah": ("sbuf", [128, 4 * C], BF), "af": ("sbuf", [128, 4 * C], BF),
+    "et": ("sbuf", [128, 4 * 192], BF), "zt": ("sbuf", [128, 4 * C], BF), "xt": ("sbuf", [128, 4 * C], BF),
+    "zq": ("sbuf", [128, C], F8), "zp": ("sbuf", [128, C], U8),
+    "xq": ("sbuf", [128, C], F8), "xp": ("sbuf", [128, C], U8),
+    "gs": ("sbuf", [128, 4 * C], F32), "sc": ("sbuf", [128, C], F32), "sb": ("sbuf", [128, B], F32),
+    "ysb": ("sbuf", [128, C], F32), "romo": ("sbuf", [128, C], F32), "romm": ("sbuf", [128, C], F32),
+}
+for _t in range(3):
+    for _n, _d in (("qe", F8), ("pe", U8), ("lq", F8), ("lp", U8)):
+        SCRATCH[_n + str(_t)] = ("sbuf", [128, EW], _d)
+    for _n, _w, _d in (("dl", 56, U16), ("tp", 352, BF), ("dr", 352, BF), ("er", 352, BF), ("bd", B, F32),
+                       ("st", 40, I32), ("sh", 40, I32), ("cur", 40, I32), ("fg", 2 * LW, BF), ("fs", 2 * LW, BF)):
+        SCRATCH[_n + str(_t)] = ("sbuf", [128, _w], _d)
+for _k in range(10):
+    SCRATCH["ra%d" % _k] = ("sbuf", [128, C], BF)
+    SCRATCH["rs%d" % _k] = ("sbuf", [128, C], BF)
+for _k in range(8):
+    SCRATCH["ps%d" % _k] = ("psum", [128, 512], F32)
+SEMAPHORES = ["vs", "ss", "ts", "gs"] + ["d%d" % k for k in range(16)] + ["arr%d" % k for k in range(3)] + ["loc%d" % k for k in range(3)]
+
+
+def rank_program(g, core, T, topo):
+    rank = T.rank_of(core)
+    if rank is None:
+        return
+    queue = {"v": g.vector, "s": g.scalar, "t": g.tensor, "g": g, "y": g.sync}
+    semof = {"v": "vs", "s": "ss", "t": "ts", "g": "gs"}
+    count = {}
+    clock = {q: {} for q in queue}
+    snap = {}
+    log = {}
+    ndma = [0]
+
+    def V(name, lo=0, hi=None, step=1):
+        return (name, lo, SCRATCH[name][1][1] if hi is None else hi, step)
+
+    def ap(v):
+        return T[v[0]][:, v[1]:v[2]:v[3]] if v[3] != 1 else T[v[0]][:, v[1]:v[2]]
+
+    def by(v):
+        return ap(v).bitcast(dt.uint8)
+
+    def ind(win, off):
+        return ap(win).indirect(ap(off))
+
+    def clash(a, b):
+        if a[1] >= b[2] or b[1] >= a[2]: return False
+        if a[3] == b[3] and a[3] > 1: return (a[1] - b[1]) % a[3] == 0
+        return True
+
+    def know(q, sem, val):
+        if clock[q].get(sem, 0) >= val: return
+        queue[q].wait_ge(T.sem[sem], val)
+        for s, n in list(snap.get((sem, val), {}).items()) + [(sem, val)]:
+            if clock[q].get(s, 0) < n: clock[q][s] = n
+
+    def order(q, reads, writes):
+        need = {}
+        for vs, isw in ((reads, False), (writes, True)):
+            for v in vs:
+                psum = v[0][:2] == "ps"
+                for (w, sem, val, oldw, oq) in log.get(v[0], ()):
+                    if (isw or oldw or (psum and oq != q)) and (psum or clash(v, w)):
+                        if need.get(sem, 0) < val: need[sem] = val
+        for sem, val in sorted(need.items(), key=lambda k: -k[1]):
+            know(q, sem, val)
+
+    def note(q, sem, val, reads, writes):
+        snap[(sem, val)] = dict(clock.get(q, {}))
+        for vs, isw in ((reads, False), (writes, True)):
+            for v in vs:
+                old = log.setdefault(v[0], [])
+                if isw:
+                    old[:] = [r for r in old if not (v[3] == 1 and v[1] <= r[0][1] and r[0][2] <= v[2])]
+                old.append((v, sem, val, isw, q))
+
+    def run(q, fn, reads, writes):
+        order(q, reads, writes)
+        s = semof[q]
+        count[s] = count.get(s, 0) + 1
+        fn().then_inc(T.sem[s], 1)
+        note(q, s, count[s], reads, writes)
+
+    def dma(q, pairs, reads, writes):
+        order(q, reads, writes)
+        s = "d%d" % ndma[0]
+        ndma[0] += 1
+        for o, i in pairs:
+            queue[q].dma_start(o, i).then_inc(T.sem[s], 16)
+        count[s] = 16 * len(pairs)
+        note(q, s, count[s], reads, writes)
+
+    def copy(out, a):
+        run("v", lambda: g.vector.tensor_copy(ap(out), ap(a)), [a], [out])
+
+    def tt(out, a, b, op):
+        run("v", lambda: g.vector.tensor_tensor(ap(out), ap(a), ap(b), op), [a, b], [out])
+
+    def ts(out, a, s1, op0, s2=None, op1=None):
+        if op1 is None:
+            run("v", lambda: g.vector.tensor_scalar(ap(out), ap(a), s1, None, op0), [a], [out])
+        else:
+            run("v", lambda: g.vector.tensor_scalar(ap(out), ap(a), s1, s2, op0, op1), [a], [out])
+
+    def tsp(out, a, col, op):
+        run("v", lambda: g.vector.tensor_scalar(ap(out), ap(a), ap(col), None, op), [a, col], [out])
+
+    def tti(out, win, off, b, op):
+        run("v", lambda: g.vector.tensor_tensor(ap(out), ind(win, off), ap(b), op), [win, off, b], [out])
+
+    def tsi(out, win, off, s1, op0):
+        run("v", lambda: g.vector.tensor_scalar(ap(out), ind(win, off), s1, None, op0), [win, off], [out])
+
+    def fill(out, c):
+        run("v", lambda: g.vector.memset(ap(out), c), [], [out])
+
+    def act(out, a, scale=1.0):
+        run("s", lambda: g.scalar.activation(ap(out), ap(a), AF.Copy, scale=scale), [a], [out])
+
+    def acti(out, win, off, scale=1.0):
+        run("s", lambda: g.scalar.activation(ap(out), ind(win, off), AF.Copy, scale=scale), [win, off], [out])
+
+    def actb(out, win, off, bias):
+        run("s", lambda: g.scalar.activation(ap(out), ind(win, off), AF.Identity, bias=bias), [win, off], [out])
+
+    def quant(q, p, a):
+        run("v", lambda: g.vector.quantize_mx(ap(q), ap(p), ap(a)), [a], [q, p])
+
+    def mm(out, l, lp, r, rp):
+        run("t", lambda: g.tensor.matmul_mx(ap(out), ap(l), ap(lp), ap(r), ap(rp), True, True), [l, lp, r, rp], [out])
+
+    def iota(out, pattern, base, cm):
+        run("g", lambda: g.iota(ap(out), pattern, base, cm, allow_small_or_imprecise_dtypes=True), [], [out])
+
+    ntb, nub, nrow = [0], [0], [0]
+
+    def tmp(n):
+        ntb[0] += n
+        return V("tb", ntb[0] - n, ntb[0])
+
+    def lst(n):
+        nub[0] += n + n % 2
+        return V("ub", nub[0] - n - n % 2, nub[0] - n % 2)
+
+    def sub(v, lo, hi, step=1):
+        if v[3] == 1: return (v[0], v[1] + lo, v[1] + hi, step)
+        return (v[0], v[1] + lo * v[3], min(v[2], v[1] + (hi - 1) * v[3] + 1), v[3] * step)
+
+    def tab(v, lo, hi):
+        return (v[0], v[1] + 16 * lo + 15, v[1] + 16 * hi, 16)
+
+    def scan(out, data):
+        h = V("hold", 0, data[2] - data[1])
+        run("v", lambda: g.vector.tensor_tensor_scan(ap(out), ap(h), ap(data), 0.0, OP.mult, OP.add), [h, data], [out])
+
+    def lookup(raw, out, win, off):
+        tti(raw, win, off, V("mask", 0, raw[2] - raw[1]), OP.mult)
+        scan(out, raw)
+
+    def look20(win, off):
+        k = nrow[0]
+        nrow[0] += 1
+        lookup(V("ra%d" % k), V("rs%d" % k), win, off)
+        return tab(V("rs%d" % k), 0, 20)
+
+    def win0(name):
+        return V(name, 16, 16 + C)
+
+    def first_of(name, k):
+        return V(name, 16 - k, 16 - k + C - 1, 2)
+
+    def second_of(name, k):
+        return V(name, 17 - k, 17 - k + C - 1, 2)
+
+    def wf(b):
+        return V("wf", b * WD, (b + 1) * WD)
+
+    def wfF(b):
+        return V("wf", b * WD, b * WD + C)
+
+    def el(b):
+        return (b, 4 * C - 3 + b, 4)
+
+    def cols(name, b, n=128):
+        return V(name, n * b, n * b + n)
+
+    dma("y", [(T.oi[:], T.o[:]), (T.mi[:], T.m[:])], [], [V("oi"), V("mi")])
+    dma("s", [(T.x0[:], T.x[:])], [], [V("x0")])
+    dma("y", [(T.ut[:], T.u[:])], [], [V("ut")])
+    dma("y", [(by(V("wq")), T.wc[:]), (T.wp[:], T.ws[:])], [], [V("wq"), V("wp")])
+    dma("y", [(T.vt[:], T.v[:])], [], [V("vt")])
+
+    iota(V("pcol"), [[0, 8]], 0, 1)
+    iota(V("kpat"), [[32, 10], [1, 2]], 0, 0)
+    iota(V("j16"), [[0, C // 16], [1, 16]], 0, 0)
+    iota(V("iota"), [[1, C]], -B, 0)
+    iota(V("uli"), [[16, 8]], 0, 0)
+    fill(V("ones"), 1.0)
+    run("g", lambda: g.affine_select(T.ect[:], T.ones[:], [[1, 516]], OP.is_equal, 0.0, -3, -4), [V("ones")], [V("ect")])
+    iota(V("cw"), [[1024, C]], -1024 * B, 0)
+    pm, pm2 = tmp(1), tmp(1)
+    ts(V("pcol2"), V("pcol"), 15, OP.bitwise_and)
+    copy(pm, V("pcol2", 0, 1))
+    ts(pm2, pm, 2.0, OP.mult)
+    K = [tmp(20), tmp(20)]
+    tsp(K[0], V("kpat"), pm2, OP.add)
+    ts(K[1], K[0], -1.0, OP.add)
+    ku0, first = lst(20), tmp(10)
+    copy(ku0, K[0])
+    ts(first, sub(K[1], 0, 20, 2), 0.0, OP.is_lt)
+    for t in range(3):
+        kA = sub(K[t % 2], 0, 20, 2)
+        ts(V("dl%d" % t, 0, 6), sub(kA, 0, 6), 0.0, OP.max)
+        ts(V("dl%d" % t, 26, 36), kA, 0.0, OP.max)
+    tsp(V("mask", 0, C), V("j16"), pm, OP.is_equal)
+    ts(V("hold", 0, C), V("j16"), 0.0, OP.is_gt)
+    copy(V("mask", C, LW), V("mask", 0, C))
+    copy(V("hold", C, LW), V("hold", 0, C))
+    fill(V("bw", 0, 1), -1e29)
+    fill(V("bw", 1, 8), 1e29)
+    fill(V("tp1", 328, 352), 0.0)
+    fill(V("dr1", 328, 352), 0.0)
+    for b in range(4):
+        fill(V("wf", b * WD + C, (b + 1) * WD), 0.0)
+    onat, mu = lst(20), [lst(20) for k in range(4)]
+    copy(onat, V("oi"))
+    copy(mu[0], V("mi"))
+
+    acti(V("orow"), V("iota"), onat)
+    acti(V("mrow"), V("iota"), mu[0])
+    run("v", lambda: g.vector.tensor_copy(ind(V("prow"), onat), ap(V("iota"))), [V("iota"), onat], [V("prow")])
+    ot = look20(V("orow"), ku0)
+    ou = lst(20)
+    ts(ou, ot, float(B), OP.add)
+    ts(V("cur0", 0, 20), ot, float(B), OP.add)
+    for b in range(4):
+        quant(cols("eq", b), cols("ep", b), V("ect", 3 - b, 515 - b))
+    quant(V("xq"), V("xp"), V("x0"))
+    xt0 = look20(V("mrow"), ou)
+    xu = lst(20)
+    ts(xu, xt0, float(B), OP.add)
+    quant(V("uq"), V("up"), V("ut"))
+    copy(V("ulu"), V("uli"))
+    run("s", lambda: g.scalar.activation(T.up16[:], T.up[:].indirect(T.ulu[:]), AF.Copy), [V("up"), V("ulu")], [V("up16")])
+    run("v", lambda: g.vector.tensor_copy(T.uq16[:].bitcast(dt.uint32), T.uq[:].bitcast(dt.uint32).indirect(T.ulu[:])), [V("uq"), V("ulu")], [V("uq16")])
+    Mt0 = look20(V("prow"), xu)
+    M0, x1 = tmp(20), tmp(20)
+    ts(M0, Mt0, float(B), OP.add)
+
+    def static(t, M):
+        k = t % 2
+        cur = V("cur%d" % t)
+        o = sub(cur, 0, 20)
+        oA, oB = sub(cur, 0, 20, 2), sub(cur, 1, 20, 2)
+        if M is None:
+            M = V("mi%d" % t)
+            ts(M, sub(cur, 20, 40), 1023, OP.bitwise_and)
+        MA, MB = sub(M, 0, 20, 2), sub(M, 1, 20, 2)
+        d, b2, y, eq, gt, S, do, d4, ix, ixu = tmp(20), tmp(20), tmp(20), tmp(10), tmp(10), tmp(10), tmp(10), tmp(10), tmp(10), lst(10)
+        bl, ok = tmp(10), lst(10)
+        tt(bl, MA, sub(K[k], 1, 20, 2), OP.is_equal)
+        if k:
+            bl2 = tmp(10)
+            tt(bl2, bl, first, OP.max)
+            bl = bl2
+        copy(ok, bl)
+        acti(V("bd%d" % t), V("bw"), ok)
+        tt(d, M, K[k], OP.is_gt)
+        ts(b2, o, float(B), OP.is_lt, 2.0, OP.mult)
+        tt(y, d, b2, OP.add)
+        tt(eq, sub(y, 0, 20, 2), sub(y, 1, 20, 2), OP.is_equal)
+        tt(gt, MA, MB, OP.is_gt)
+        tt(S, eq, gt, OP.mult)
+        tt(do, oB, oA, OP.subtract)
+        ts(d4, do, float(B), OP.add)
+        tt(ix, d4, S, OP.mult)
+        copy(ixu, ix)
+        acti(first_of("dr%d" % t, k), V("cw"), ixu)
+        acti(second_of("dr%d" % t, k), V("cw"), ixu)
+        return dict(t=t, do=do, S=S, M=M, oA=oA, oB=oB)
+
+    def static2(r):
+        copy(V("dl%d" % r["t"], 6, 26), r["M"])
+        r["oAu"], r["oBu"], r["nS"] = lst(10), lst(10), tmp(10)
+        copy(r["oBu"], r["oB"])
+        copy(r["oAu"], r["oA"])
+        ts(r["nS"], r["S"], -1.0, OP.mult, 1.0, OP.add)
+        r["D"] = look20(win0("dr%d" % r["t"]), V("dl%d" % r["t"], 6, 26))
+
+    def products(t):
+        mm(V("ps4", 0, C), V("uq16"), V("up16"), V("xq"), V("xp"))
+        for b in range(4):
+            mm(V("ps%d" % b, 0, C), cols("eq", b), cols("ep", b), V("xq"), V("xp"))
+        act(V("sc"), V("ps4", 0, C))
+        for b in range(4):
+            act(wfF(b), V("ps%d" % b, 0, C), 0.5)
+
+    fill(V("cw", 0, 1), 1.0)
+    r = static(0, M0)
+    ts(x1, xt0, 1024.0, OP.mult, 1024.0 * B, OP.add)
+    tt(V("cur0", 20, 40), x1, M0, OP.add)
+    products(0)
+    static2(r)
+    P = None
+    for t in range(3):
+        k = t % 2
+        nl = 5 + k
+        nu = 10 - nl
+        dl, tp, er = "dl%d" % t, "tp%d" % t, "er%d" % t
+        cur, st = V("cur%d" % t), V("st%d" % t)
+        val = sub(cur, 20, 40)
+        D, nS, do = r["D"], r["nS"], r["do"]
+        tti(V("sb"), V("sc"), r["oBu"], V("bd%d" % t), OP.max)
+        tti(first_of(tp, k), V("sc"), r["oAu"], V("sb"), OP.is_gt)
+        ts(second_of(tp, k), first_of(tp, k), -1.0, OP.mult)
+        fg, fs = "fg%d" % t, "fs%d" % t
+        eu = lst(20)
+
+        def renew(tc, tM, c0, c1):
+            n = c1 - c0
+            d1, alt, rr, dd, d2 = tmp(2 * n), tmp(2 * n), tmp(n), tmp(n), tmp(n)
+            tt(d1, tM, sub(D, 2 * c0, 2 * c1), OP.mult)
+            tt(rr, tc, sub(nS, c0, c1), OP.mult)
+            tt(alt, d1, sub(val, 2 * c0, 2 * c1), OP.add)
+            aA, aB = sub(alt, 0, 2 * n, 2), sub(alt, 1, 2 * n, 2)
+            tt(dd, aB, aA, OP.subtract)
+            tt(d2, dd, rr, OP.mult)
+            eA, eB = sub(st, 20 + 2 * c0, 20 + 2 * c1, 2), sub(st, 21 + 2 * c0, 20 + 2 * c1, 2)
+            tt(eA, aA, d2, OP.add)
+            tt(eB, aB, d2, OP.subtract)
+            ts(sub(eu, c0, c1), eA, 1.0 / 1024, OP.mult)
+            ts(sub(eu, 10 + c0, 10 + c1), eB, 1.0 / 1024, OP.mult)
+
+        wl = 16 * (6 + 2 * nl)
+        fl = V(fs, 0, wl)
+        lookup(V(fg, 0, wl), fl, win0(tp), V(dl, 0, 6 + 2 * nl))
+        renew(tab(fl, 0, nl), tab(fl, 6, 6 + 2 * nl), 0, nl)
+        for b in range(4):
+            acti(V("et", b, 128 * nl - 7 + b, 8), wfF(b), sub(eu, 0, nl), 2.0)
+            tsi(V("et", 4 + b, 128 * nl - 3 + b, 8), wfF(b), sub(eu, 10, 10 + nl), 2.0, OP.mult)
+        ne = NE[t]
+        qe, pe, lq, lp = [V(s + str(t), 0, ne) for s in ("qe", "pe", "lq", "lp")]
+        quant(qe, pe, V("et", 0, 4 * ne))
+        dst = T.cores[rank ^ STEP[t]]
+        rid, pid = topo.addr(dst)[:2]
+        arr, loc, full = "arr%d" % t, "loc%d" % t, 2 * len(topo.engines(core, dst))
+        order("g", [qe, pe], [])
+        g.remote_dma(by(lq), by(qe), T.sem[arr], T.sem[loc], pid, rid, topo.mask(core, dst))
+        g.remote_dma(ap(lp), ap(pe), T.sem[arr], T.sem[loc], pid, rid, topo.mask(core, dst))
+        count[arr] = count[loc] = full
+        note("g", loc, full, [qe, pe], [])
+        log["lq%d" % t] = [(lq, arr, full, True, "r")]
+        log["lp%d" % t] = [(lp, arr, full, True, "r")]
+        for b in range(4):
+            acti(cols("ah", b, C), wfF(b), mu[t])
+        if t == 0:
+            tt(V("ra8"), V("prow"), V("mask", 0, C), OP.mult)
+            scan(V("rs8"), V("ra8"))
+            p0 = tab(V("rs8"), 0, 20)
+            ts(V("dl0", 36, 56), p0, float(B), OP.add)
+            P = tmp(20)
+            ts(P, p0, float(B - PB), OP.add)
+        wu = 16 * (2 * nu + 30)
+        lu = 6 + 2 * nl
+        fu = V(fs, LW, LW + wu)
+        lookup(V(fg, LW, LW + wu), fu, win0(tp), V(dl, lu, lu + 2 * nu + 30))
+        tc = tab(fu, 2 * nu, 2 * nu + 10)
+        renew(sub(tc, nl, 10), tab(fu, 0, 2 * nu), nl, 10)
+        acti(first_of(er, k), V("iota"), sub(eu, 0, 10))
+        acti(second_of(er, k), V("iota"), sub(eu, 10, 20))
+        if k: act(V(er, 16 + C - 1, 16 + C), V(er, 15, 16))
+        pn, pf, pz, pu = tmp(20), tmp(20), tmp(20), lst(20) if t == 2 else V("dl%d" % (t + 1), 36, 56)
+        tt(pn, P, tab(fu, 2 * nu + 10, 2 * nu + 30), OP.add)
+        P = pn
+        ts(pu, pn, float(PB), OP.add)
+        t1 = tmp(10)
+        tt(t1, tc, do, OP.mult)
+        tt(sub(st, 0, 20, 2), sub(cur, 0, 20, 2), t1, OP.add)
+        tt(sub(st, 1, 20, 2), sub(cur, 1, 20, 2), t1, OP.subtract)
+        ts(pf, pn, float(B - PB), OP.is_lt, 1000.0, OP.mult)
+        tt(pz, pf, pn, OP.add)
+        if t == 2:
+            ofu = lst(20)
+            copy(sub(ofu, 0, 10), sub(st, 0, 20, 2))
+            copy(sub(ofu, 10, 20), sub(st, 1, 20, 2))
+        mn = look20(win0(er), pu)
+        vm, vl = tmp(20), lst(20)
+        tt(vm, pz, mn, OP.max)
+        ts(vl, vm, float(B), OP.add)
+        if t < 2:
+            s, h = T["st%d" % t], T["sh%d" % t]
+            pairs = []
+            if t == 0:
+                for q in range(0, 128, 16):
+                    pairs.append((h[q + 1:q + 16, :], s[q:q + 15, :]))
+                for z in (0, 20):
+                    pairs.append((h[0:128:16, z + 2:z + 20], s[15:128:16, z:z + 18]))
+                    pairs.append((h[0:128:16, z:z + 2], s[15:128:16, z + 18:z + 20]))
+            else:
+                for q in range(0, 128, 16):
+                    pairs.append((h[q:q + 15, :], s[q + 1:q + 16, :]))
+                for z in (0, 20):
+                    pairs.append((h[15:128:16, z:z + 18], s[0:128:16, z + 2:z + 20]))
+                    pairs.append((h[15:128:16, z + 18:z + 20], s[0:128:16, z:z + 2]))
+            dma("y", pairs, [st], [V("sh%d" % t)])
+        for b in range(4):
+            mm(V("ps%d" % b, 0, ne), cols("eq", b), cols("ep", b), lq, lp)
+            act(V("wf", b * WD + C + 1 - k, b * WD + C + 1 - k + ne), V("ps%d" % b, 0, ne), 0.5)
+        for b in range(4):
+            tti(V("zt", *el(b)), wf(b), vl, cols("ah", b, C), OP.add)
+        act(V("af"), V("ah"), 2.0)
+        quant(V("zq"), V("zp"), V("zt"))
+        ts(mu[t + 1], mn, float(B), OP.add)
+        if t == 2:
+            actb(V("romo", 0, C - 1, 2), V("iota"), sub(ofu, 0, 10), float(B))
+            actb(V("romo", 1, C, 2), V("iota"), sub(ofu, 10, 20), float(B))
+        for b in range(4):
+            mm(V("ps%d" % (4 + b), 0, C), cols("wq", b), cols("wp", b), V("zq"), V("zp"))
+            act(cols("gs", b, C), V("ps%d" % (4 + b), 0, C), 0.0078125)
+        if t < 2:
+            n, h = "cur%d" % (t + 1), "sh%d" % t
+            if t == 0:
+                copy(V(n, 0, 39, 2), V(h, 1, 40, 2))
+                copy(V(n, 1, 40, 2), sub(st, 0, 39, 2))
+            else:
+                copy(V(n, 0, 39, 2), sub(st, 1, 40, 2))
+                copy(V(n, 1, 40, 2), V(h, 0, 39, 2))
+            r = static(t + 1, None)
+        else:
+            quant(V("vq"), V("vp"), V("vt"))
+        for b in range(4):
+            tti(V("xt", *el(b)), cols("gs", b, C), mu[t + 1], cols("af", b, C), OP.add)
+        quant(V("xq"), V("xp"), V("xt"))
+        if t < 2:
+            products(t + 1)
+            static2(r)
+    mm(V("ps4", 0, C), V("vq"), V("vp"), V("xq"), V("xp"))
+    dma("y", [(T.oc[:], by(V("xq")))] + [(T.osc[4 * q:4 * q + 4, :], T.xp[32 * q:32 * q + 4, :]) for q in range(4)], [V("xq"), V("xp")], [])
+    act(V("ysb"), V("ps4", 0, C))
+    dma("s", [(T.y[:], T.ysb[:])], [V("ysb")], [])
+    actb(V("romm"), V("iota"), mu[3], float(B))
+    dma("y", [(T.om[:, 0:C], T.romo[0:128:16, :]), (T.om[:, C:2 * C], T.romm[0:128:16, :])], [V("romo"), V("romm")], [])
+    for sem, n in count.items():
+        know("g", sem, n)
+
+
+SCRATCH["mi1"] = ("sbuf", [128, 20], I32)
+SCRATCH["mi2"] = ("sbuf", [128, 20], I32)

@@ -1,3 +1,5 @@
+import math
+import numpy as np
 from concourse.mybir import dt, AluOpType as OP, ActivationFunctionType as AF
 
 C, B = 320, 160
@@ -6,6 +8,7 @@ EW = 176
 WD = C + EW
 NE = [160, 162, 160]
 F8, BF, F32, U16, U8, I32 = "float8_e4m3fn_x4", "bfloat16", "float32", "uint16", "uint8", "int32"
+CYCLE = 0.00104
 LW = 640
 PB = 839
 
@@ -18,7 +21,7 @@ SCRATCH = {
     "vq": ("sbuf", [128, 128], F8), "vp": ("sbuf", [128, 128], U8),
     "ect": ("sbuf", [128, 516], BF), "ones": ("sbuf", [128, 516], BF),
     "eq": ("sbuf", [128, 512], F8), "ep": ("sbuf", [128, 512], U8),
-    "iota": ("sbuf", [128, C], BF), "cw": ("sbuf", [128, C], BF), "bw": ("sbuf", [128, 8], F32),
+    "iota": ("sbuf", [128, C], BF), "cw": ("sbuf", [128, C], BF), "bw": ("sbuf", [128, B + 8], F32),
     "j16": ("sbuf", [128, C], BF), "mask": ("sbuf", [128, LW], BF), "hold": ("sbuf", [128, LW], BF),
     "pcol": ("sbuf", [128, 8], I32), "pcol2": ("sbuf", [128, 8], I32), "uli": ("sbuf", [128, 8], I32), "ulu": ("sbuf", [128, 8], U16),
     "kpat": ("sbuf", [128, 20], F32),
@@ -36,7 +39,7 @@ for _t in range(3):
     for _n, _d in (("qe", F8), ("pe", U8), ("lq", F8), ("lp", U8)):
         SCRATCH[_n + str(_t)] = ("sbuf", [128, EW], _d)
     for _n, _w, _d in (("dl", 56, U16), ("tp", 352, BF), ("dr", 352, BF), ("er", 352, BF), ("bd", B, F32),
-                       ("st", 40, I32), ("sh", 40, I32), ("cur", 40, I32), ("fg", 2 * LW, BF), ("fs", 2 * LW, BF)):
+                       ("st", 80, I32), ("sh", 80, I32), ("cur", 80, I32), ("fg", 2 * LW, BF), ("fs", 2 * LW, BF)):
         SCRATCH[_n + str(_t)] = ("sbuf", [128, _w], _d)
 for _k in range(10):
     SCRATCH["ra%d" % _k] = ("sbuf", [128, C], BF)
@@ -101,27 +104,48 @@ def rank_program(g, core, T, topo):
                     old[:] = [r for r in old if not (v[3] == 1 and v[1] <= r[0][1] and r[0][2] <= v[2])]
                 old.append((v, sem, val, isw, q))
 
-    def run(q, fn, reads, writes):
-        order(q, reads, writes)
-        s = semof[q]
-        count[s] = count.get(s, 0) + 1
-        fn().then_inc(T.sem[s], 1)
-        note(q, s, count[s], reads, writes)
+    calls = []
+
+    def put(q, issue, reads, writes, cost, late=0.0):
+        calls.append((q, issue, reads, writes, cost, late))
+
+    def run(q, fn, reads, writes, kind=""):
+        def issue():
+            order(q, reads, writes)
+            s = semof[q]
+            count[s] = count.get(s, 0) + 1
+            fn().then_inc(T.sem[s], 1)
+            note(q, s, count[s], reads, writes)
+        o = writes[0]
+        n = (o[2] - o[1] + o[3] - 1) // o[3]
+        narrow = all(SCRATCH[v[0]][2] in (BF, U16) for v in reads + writes)
+        psum = any(v[0][:2] == "ps" for v in reads)
+        if kind == "ind": c = 0.055 + 1.56 * CYCLE * n
+        elif kind == "scat": c = 3.5 * CYCLE * n
+        elif kind == "q": c = 0.015 + 4 * 0.00028 * n
+        elif q == "t": c = (n + 16) * CYCLE * 1.2
+        elif q == "g": c = 0.17 + 2 * CYCLE * n
+        elif q == "s": c = CYCLE * max(n, 64) + 0.1
+        else: c = CYCLE * max(64, n * (2 if kind == "tt" and not psum else 0.5 if narrow else 1))
+        put(q, issue, reads, writes, c)
 
     def dma(q, pairs, reads, writes):
-        order(q, reads, writes)
-        s = "d%d" % ndma[0]
-        ndma[0] += 1
-        for o, i in pairs:
-            queue[q].dma_start(o, i).then_inc(T.sem[s], 16)
-        count[s] = 16 * len(pairs)
-        note(q, s, count[s], reads, writes)
+        def issue():
+            order(q, reads, writes)
+            s = "d%d" % ndma[0]
+            ndma[0] += 1
+            for o, i in pairs:
+                queue[q].dma_start(o, i).then_inc(T.sem[s], 16)
+            count[s] = 16 * len(pairs)
+            note(q, s, count[s], reads, writes)
+        big = writes and SCRATCH[writes[0][0]][1][1] > 500
+        put(q, issue, reads, writes, 0.07 * len(pairs), 4.0 if big else 2.2)
 
     def copy(out, a):
         run("v", lambda: g.vector.tensor_copy(ap(out), ap(a)), [a], [out])
 
     def tt(out, a, b, op):
-        run("v", lambda: g.vector.tensor_tensor(ap(out), ap(a), ap(b), op), [a, b], [out])
+        run("v", lambda: g.vector.tensor_tensor(ap(out), ap(a), ap(b), op), [a, b], [out], "tt")
 
     def ts(out, a, s1, op0, s2=None, op1=None):
         if op1 is None:
@@ -133,10 +157,10 @@ def rank_program(g, core, T, topo):
         run("v", lambda: g.vector.tensor_scalar(ap(out), ap(a), ap(col), None, op), [a, col], [out])
 
     def tti(out, win, off, b, op):
-        run("v", lambda: g.vector.tensor_tensor(ap(out), ind(win, off), ap(b), op), [win, off, b], [out])
+        run("v", lambda: g.vector.tensor_tensor(ap(out), ind(win, off), ap(b), op), [win, off, b], [out], "ind")
 
     def tsi(out, win, off, s1, op0):
-        run("v", lambda: g.vector.tensor_scalar(ap(out), ind(win, off), s1, None, op0), [win, off], [out])
+        run("v", lambda: g.vector.tensor_scalar(ap(out), ind(win, off), s1, None, op0), [win, off], [out], "ind")
 
     def fill(out, c):
         run("v", lambda: g.vector.memset(ap(out), c), [], [out])
@@ -145,13 +169,13 @@ def rank_program(g, core, T, topo):
         run("s", lambda: g.scalar.activation(ap(out), ap(a), AF.Copy, scale=scale), [a], [out])
 
     def acti(out, win, off, scale=1.0):
-        run("s", lambda: g.scalar.activation(ap(out), ind(win, off), AF.Copy, scale=scale), [win, off], [out])
+        run("s", lambda: g.scalar.activation(ap(out), ind(win, off), AF.Copy, scale=scale), [win, off], [out], "ind")
 
     def actb(out, win, off, bias):
-        run("s", lambda: g.scalar.activation(ap(out), ind(win, off), AF.Identity, bias=bias), [win, off], [out])
+        run("s", lambda: g.scalar.activation(ap(out), ind(win, off), AF.Identity, bias=bias), [win, off], [out], "ind")
 
     def quant(q, p, a):
-        run("v", lambda: g.vector.quantize_mx(ap(q), ap(p), ap(a)), [a], [q, p])
+        run("v", lambda: g.vector.quantize_mx(ap(q), ap(p), ap(a)), [a], [q, p], "q")
 
     def mm(out, l, lp, r, rp):
         run("t", lambda: g.tensor.matmul_mx(ap(out), ap(l), ap(lp), ap(r), ap(rp), True, True), [l, lp, r, rp], [out])
@@ -235,27 +259,28 @@ def rank_program(g, core, T, topo):
     ku0, first = lst(20), tmp(10)
     copy(ku0, K[0])
     ts(first, sub(K[1], 0, 20, 2), 0.0, OP.is_lt)
+    last, K2 = tmp(20), tmp(20)
+    ts(last, K[1], 0.0, OP.is_lt, float(C), OP.mult)
+    tt(K2, K[1], last, OP.add)
     for t in range(3):
         kA = sub(K[t % 2], 0, 20, 2)
         ts(V("dl%d" % t, 0, 6), sub(kA, 0, 6), 0.0, OP.max)
         ts(V("dl%d" % t, 26, 36), kA, 0.0, OP.max)
     tsp(V("mask", 0, C), V("j16"), pm, OP.is_equal)
-    ts(V("hold", 0, C), V("j16"), 0.0, OP.is_gt)
-    copy(V("mask", C, LW), V("mask", 0, C))
-    copy(V("hold", C, LW), V("hold", 0, C))
-    fill(V("bw", 0, 1), -1e29)
-    fill(V("bw", 1, 8), 1e29)
-    fill(V("tp1", 328, 352), 0.0)
-    fill(V("dr1", 328, 352), 0.0)
-    for b in range(4):
-        fill(V("wf", b * WD + C, (b + 1) * WD), 0.0)
+    run("s", lambda: g.scalar.activation(ap(V("hold", 0, C)), T.j16[:], AF.Sign), [V("j16")], [V("hold", 0, C)])
+    act(V("mask", C, LW), V("mask", 0, C))
+    act(V("hold", C, LW), V("hold", 0, C))
+    for v, z in ((V("bw", 0, B + 1), -1e29), (V("bw", B + 1, B + 8), 1e29)):
+        run("s", lambda v=v, z=z: g.scalar.activation(ap(v), ap(V("j16", 0, v[2] - v[1])), AF.Identity, bias=z, scale=0.0), [V("j16")], [v])
+    for v in [V("tp1", 328, 352), V("dr1", 328, 352)] + [V("wf", b * WD + C, (b + 1) * WD) for b in range(4)]:
+        act(v, V("j16", 0, v[2] - v[1]), 0.0)
     onat, mu = lst(20), [lst(20) for k in range(4)]
     copy(onat, V("oi"))
     copy(mu[0], V("mi"))
 
     acti(V("orow"), V("iota"), onat)
     acti(V("mrow"), V("iota"), mu[0])
-    run("v", lambda: g.vector.tensor_copy(ind(V("prow"), onat), ap(V("iota"))), [V("iota"), onat], [V("prow")])
+    run("v", lambda: g.vector.tensor_copy(ind(V("prow"), onat), ap(V("iota"))), [V("iota"), onat], [V("prow")], "scat")
     ot = look20(V("orow"), ku0)
     ou = lst(20)
     ts(ou, ot, float(B), OP.add)
@@ -268,50 +293,51 @@ def rank_program(g, core, T, topo):
     ts(xu, xt0, float(B), OP.add)
     quant(V("uq"), V("up"), V("ut"))
     copy(V("ulu"), V("uli"))
-    run("s", lambda: g.scalar.activation(T.up16[:], T.up[:].indirect(T.ulu[:]), AF.Copy), [V("up"), V("ulu")], [V("up16")])
-    run("v", lambda: g.vector.tensor_copy(T.uq16[:].bitcast(dt.uint32), T.uq[:].bitcast(dt.uint32).indirect(T.ulu[:])), [V("uq"), V("ulu")], [V("uq16")])
+    run("s", lambda: g.scalar.activation(T.up16[:], T.up[:].indirect(T.ulu[:]), AF.Copy), [V("up"), V("ulu")], [V("up16")], "ind")
+    run("v", lambda: g.vector.tensor_copy(T.uq16[:].bitcast(dt.uint32), T.uq[:].bitcast(dt.uint32).indirect(T.ulu[:])), [V("uq"), V("ulu")], [V("uq16")], "ind")
     Mt0 = look20(V("prow"), xu)
     M0, x1 = tmp(20), tmp(20)
     ts(M0, Mt0, float(B), OP.add)
+
+    def sides(y, M, o, k):
+        d, b2 = tmp(20), tmp(20)
+        tt(d, M, (K[0], K2)[k], OP.is_gt)
+        ts(b2, o, float(B), OP.is_lt, 2.0, OP.mult)
+        tt(y, d, b2, OP.add)
 
     def static(t, M):
         k = t % 2
         cur = V("cur%d" % t)
         o = sub(cur, 0, 20)
         oA, oB = sub(cur, 0, 20, 2), sub(cur, 1, 20, 2)
-        if M is None:
-            M = V("mi%d" % t)
-            ts(M, sub(cur, 20, 40), 1023, OP.bitwise_and)
+        y = sub(cur, 40, 60)
+        if M is None: M = sub(cur, 60, 80)
+        else: sides(y, M, o, 0)
         MA, MB = sub(M, 0, 20, 2), sub(M, 1, 20, 2)
-        d, b2, y, eq, gt, S, do, d4, ix, ixu = tmp(20), tmp(20), tmp(20), tmp(10), tmp(10), tmp(10), tmp(10), tmp(10), tmp(10), lst(10)
-        bl, ok = tmp(10), lst(10)
-        tt(bl, MA, sub(K[k], 1, 20, 2), OP.is_equal)
+        eq, gt, S, do, bi, biu = tmp(10), tmp(10), tmp(10), tmp(10), tmp(20), lst(20)
+        ix, ixu = sub(bi, 10, 20), sub(biu, 10, 20)
         if k:
-            bl2 = tmp(10)
-            tt(bl2, bl, first, OP.max)
-            bl = bl2
-        copy(ok, bl)
-        acti(V("bd%d" % t), V("bw"), ok)
-        tt(d, M, K[k], OP.is_gt)
-        ts(b2, o, float(B), OP.is_lt, 2.0, OP.mult)
-        tt(y, d, b2, OP.add)
+            bl = tmp(10)
+            tt(bl, MA, sub(K[k], 1, 20, 2), OP.is_equal)
+            tt(sub(bi, 0, 10), bl, first, OP.max)
+        else:
+            tt(sub(bi, 0, 10), MA, sub(K[k], 1, 20, 2), OP.is_equal)
         tt(eq, sub(y, 0, 20, 2), sub(y, 1, 20, 2), OP.is_equal)
         tt(gt, MA, MB, OP.is_gt)
         tt(S, eq, gt, OP.mult)
         tt(do, oB, oA, OP.subtract)
-        ts(d4, do, float(B), OP.add)
-        tt(ix, d4, S, OP.mult)
-        copy(ixu, ix)
+        tt(ix, do, S, OP.mult)
+        ts(biu, bi, float(B), OP.add)
+        acti(V("bd%d" % t), V("bw"), sub(biu, 0, 10))
         acti(first_of("dr%d" % t, k), V("cw"), ixu)
         acti(second_of("dr%d" % t, k), V("cw"), ixu)
         return dict(t=t, do=do, S=S, M=M, oA=oA, oB=oB)
 
     def static2(r):
         copy(V("dl%d" % r["t"], 6, 26), r["M"])
-        r["oAu"], r["oBu"], r["nS"] = lst(10), lst(10), tmp(10)
+        r["oAu"], r["oBu"] = lst(10), lst(10)
         copy(r["oBu"], r["oB"])
         copy(r["oAu"], r["oA"])
-        ts(r["nS"], r["S"], -1.0, OP.mult, 1.0, OP.add)
         r["D"] = look20(win0("dr%d" % r["t"]), V("dl%d" % r["t"], 6, 26))
 
     def products(t):
@@ -322,7 +348,7 @@ def rank_program(g, core, T, topo):
         for b in range(4):
             act(wfF(b), V("ps%d" % b, 0, C), 0.5)
 
-    fill(V("cw", 0, 1), 1.0)
+    fill(V("cw", B, B + 1), 1.0)
     r = static(0, M0)
     ts(x1, xt0, 1024.0, OP.mult, 1024.0 * B, OP.add)
     tt(V("cur0", 20, 40), x1, M0, OP.add)
@@ -336,7 +362,7 @@ def rank_program(g, core, T, topo):
         dl, tp, er = "dl%d" % t, "tp%d" % t, "er%d" % t
         cur, st = V("cur%d" % t), V("st%d" % t)
         val = sub(cur, 20, 40)
-        D, nS, do = r["D"], r["nS"], r["do"]
+        D, S, do = r["D"], r["S"], r["do"]
         tti(V("sb"), V("sc"), r["oBu"], V("bd%d" % t), OP.max)
         tti(first_of(tp, k), V("sc"), r["oAu"], V("sb"), OP.is_gt)
         ts(second_of(tp, k), first_of(tp, k), -1.0, OP.mult)
@@ -347,7 +373,7 @@ def rank_program(g, core, T, topo):
             n = c1 - c0
             d1, alt, rr, dd, d2 = tmp(2 * n), tmp(2 * n), tmp(n), tmp(n), tmp(n)
             tt(d1, tM, sub(D, 2 * c0, 2 * c1), OP.mult)
-            tt(rr, tc, sub(nS, c0, c1), OP.mult)
+            tt(rr, tc, sub(S, c0, c1), OP.is_gt)
             tt(alt, d1, sub(val, 2 * c0, 2 * c1), OP.add)
             aA, aB = sub(alt, 0, 2 * n, 2), sub(alt, 1, 2 * n, 2)
             tt(dd, aB, aA, OP.subtract)
@@ -371,13 +397,17 @@ def rank_program(g, core, T, topo):
         dst = T.cores[rank ^ STEP[t]]
         rid, pid = topo.addr(dst)[:2]
         arr, loc, full = "arr%d" % t, "loc%d" % t, 2 * len(topo.engines(core, dst))
-        order("g", [qe, pe], [])
-        g.remote_dma(by(lq), by(qe), T.sem[arr], T.sem[loc], pid, rid, topo.mask(core, dst))
-        g.remote_dma(ap(lp), ap(pe), T.sem[arr], T.sem[loc], pid, rid, topo.mask(core, dst))
-        count[arr] = count[loc] = full
-        note("g", loc, full, [qe, pe], [])
-        log["lq%d" % t] = [(lq, arr, full, True, "r")]
-        log["lp%d" % t] = [(lp, arr, full, True, "r")]
+
+        def send(qe=qe, pe=pe, lq=lq, lp=lp, pid=pid, rid=rid, arr=arr, loc=loc, full=full, mask=topo.mask(core, dst)):
+            order("g", [qe, pe], [])
+            g.remote_dma(by(lq), by(qe), T.sem[arr], T.sem[loc], pid, rid, mask)
+            g.remote_dma(ap(lp), ap(pe), T.sem[arr], T.sem[loc], pid, rid, mask)
+            count[arr] = count[loc] = full
+            note("g", loc, full, [qe, pe], [])
+            log[lq[0]] = [(lq, arr, full, True, "r")]
+            log[lp[0]] = [(lp, arr, full, True, "r")]
+
+        put("g", send, [qe, pe], [lq, lp], 1.0, 2.2)
         for b in range(4):
             acti(cols("ah", b, C), wfF(b), mu[t])
         if t == 0:
@@ -387,17 +417,18 @@ def rank_program(g, core, T, topo):
             ts(V("dl0", 36, 56), p0, float(B), OP.add)
             P = tmp(20)
             ts(P, p0, float(B - PB), OP.add)
-        wu = 16 * (2 * nu + 30)
-        lu = 6 + 2 * nl
-        fu = V(fs, LW, LW + wu)
-        lookup(V(fg, LW, LW + wu), fu, win0(tp), V(dl, lu, lu + 2 * nu + 30))
-        tc = tab(fu, 2 * nu, 2 * nu + 10)
-        renew(sub(tc, nl, 10), tab(fu, 0, 2 * nu), nl, 10)
+        wu, lu = 16 * (2 * nu + 10), 6 + 2 * nl
+        fv = V(fs, LW - C, LW - C + wu)
+        lookup(V(fg, LW - C, LW - C + wu), fv, win0(tp), V(dl, lu, lu + 2 * nu + 10))
+        tc = tab(fv, 2 * nu, 2 * nu + 10)
+        renew(sub(tc, nl, 10), tab(fv, 0, 2 * nu), nl, 10)
+        fu = V(fs, LW, LW + C)
+        lookup(V(fg, LW, LW + C), fu, win0(tp), V(dl, 36, 56))
         acti(first_of(er, k), V("iota"), sub(eu, 0, 10))
         acti(second_of(er, k), V("iota"), sub(eu, 10, 20))
         if k: act(V(er, 16 + C - 1, 16 + C), V(er, 15, 16))
         pn, pf, pz, pu = tmp(20), tmp(20), tmp(20), lst(20) if t == 2 else V("dl%d" % (t + 1), 36, 56)
-        tt(pn, P, tab(fu, 2 * nu + 10, 2 * nu + 30), OP.add)
+        tt(pn, P, tab(fu, 0, 20), OP.add)
         P = pn
         ts(pu, pn, float(PB), OP.add)
         t1 = tmp(10)
@@ -415,18 +446,20 @@ def rank_program(g, core, T, topo):
         tt(vm, pz, mn, OP.max)
         ts(vl, vm, float(B), OP.add)
         if t < 2:
+            ts(sub(st, 60, 80), sub(st, 20, 40), 1023, OP.bitwise_and)
+            sides(sub(st, 40, 60), sub(st, 60, 80), sub(st, 0, 20), k)
             s, h = T["st%d" % t], T["sh%d" % t]
             pairs = []
             if t == 0:
                 for q in range(0, 128, 16):
                     pairs.append((h[q + 1:q + 16, :], s[q:q + 15, :]))
-                for z in (0, 20):
+                for z in (0, 20, 40, 60):
                     pairs.append((h[0:128:16, z + 2:z + 20], s[15:128:16, z:z + 18]))
                     pairs.append((h[0:128:16, z:z + 2], s[15:128:16, z + 18:z + 20]))
             else:
                 for q in range(0, 128, 16):
                     pairs.append((h[q:q + 15, :], s[q + 1:q + 16, :]))
-                for z in (0, 20):
+                for z in (0, 20, 40, 60):
                     pairs.append((h[15:128:16, z:z + 18], s[0:128:16, z + 2:z + 20]))
                     pairs.append((h[15:128:16, z + 18:z + 20], s[0:128:16, z:z + 2]))
             dma("y", pairs, [st], [V("sh%d" % t)])
@@ -447,11 +480,11 @@ def rank_program(g, core, T, topo):
         if t < 2:
             n, h = "cur%d" % (t + 1), "sh%d" % t
             if t == 0:
-                copy(V(n, 0, 39, 2), V(h, 1, 40, 2))
-                copy(V(n, 1, 40, 2), sub(st, 0, 39, 2))
+                copy(V(n, 0, 79, 2), V(h, 1, 80, 2))
+                copy(V(n, 1, 80, 2), V("st0", 0, 79, 2))
             else:
-                copy(V(n, 0, 39, 2), sub(st, 1, 40, 2))
-                copy(V(n, 1, 40, 2), V(h, 0, 39, 2))
+                copy(V(n, 0, 79, 2), V("st1", 1, 80, 2))
+                copy(V(n, 1, 80, 2), V(h, 0, 79, 2))
             r = static(t + 1, None)
         else:
             quant(V("vq"), V("vp"), V("vt"))
@@ -461,15 +494,107 @@ def rank_program(g, core, T, topo):
         if t < 2:
             products(t + 1)
             static2(r)
-    mm(V("ps4", 0, C), V("vq"), V("vp"), V("xq"), V("xp"))
+    for z in range(2):
+        mm(V("ps%d" % (4 + z), 0, B), V("vq"), V("vp"), V("xq", B * z, B * z + B), V("xp", B * z, B * z + B))
     dma("y", [(T.oc[:], by(V("xq")))] + [(T.osc[4 * q:4 * q + 4, :], T.xp[32 * q:32 * q + 4, :]) for q in range(4)], [V("xq"), V("xp")], [])
-    act(V("ysb"), V("ps4", 0, C))
-    dma("s", [(T.y[:], T.ysb[:])], [V("ysb")], [])
+    act(V("ysb", 0, B), V("ps4", 0, B))
+    copy(V("ysb", B, C), V("ps5", 0, B))
+    dma("s", [(T.y[:, 0:B], T.ysb[:, 0:B])], [V("ysb", 0, B)], [])
+    dma("s", [(T.y[:, B:C], T.ysb[:, B:C])], [V("ysb", B, C)], [])
     actb(V("romm"), V("iota"), mu[3], float(B))
     dma("y", [(T.om[:, 0:C], T.romo[0:128:16, :]), (T.om[:, C:2 * C], T.romm[0:128:16, :])], [V("romo"), V("romm")], [])
+    if "plan" not in PLAN:
+        seen, before = {}, []
+        for i, (q, issue, reads, writes, cost, late) in enumerate(calls):
+            p = set()
+            for vs, isw in ((reads, False), (writes, True)):
+                for v in vs:
+                    psum = v[0][:2] == "ps"
+                    for w, j, oldw in seen.get(v[0], ()):
+                        if (isw or oldw or (psum and calls[j][0] != q)) and (psum or clash(v, w)): p.add(j)
+            for vs, isw in ((reads, False), (writes, True)):
+                for v in vs: seen.setdefault(v[0], []).append((v, i, isw))
+            before.append(sorted(p))
+        PLAN["plan"] = plan([(c[0], c[4], c[5]) for c in calls], before)
+    for i in PLAN["plan"]:
+        calls[i][1]()
     for sem, n in count.items():
         know("g", sem, n)
 
 
-SCRATCH["mi1"] = ("sbuf", [128, 20], I32)
-SCRATCH["mi2"] = ("sbuf", [128, 20], I32)
+PLAN = {}
+MACHINES = [(1.0, 0.06, 0.0, 0.0), (1.1, 0.1, 0.06, 0.5), (1.2, 0.15, 0.1, 1.0), (0.9, 0.08, 0.05, 2.0)]
+TRIES = 170000
+
+
+def walk(ops, before, seqs, m):
+    fac, wake, own, more = m
+    end, at, free = {}, {q: 0 for q in seqs}, {q: 0.0 for q in seqs}
+    begun = {}
+    left = len(ops)
+    while left:
+        moved = False
+        for q, seq in seqs.items():
+            while at[q] < len(seq):
+                i = seq[at[q]]
+                t, late = free[q], False
+                ok = True
+                for j in before[i]:
+                    if j not in end:
+                        ok = False
+                        break
+                if not ok: break
+                for j in before[i]:
+                    e = end[j] + (own if ops[j][0] == q and end[j] >= free[q] - 1e-9 else wake if ops[j][0] != q and end[j] > free[q] else 0.0)
+                    if e > t: t = e
+                begun[i] = t
+                free[q] = t + ops[i][1] * (fac if q in "vs" else 1.0)
+                end[i] = free[q] + (ops[i][2] + more if ops[i][2] else 0.0)
+                at[q] += 1
+                left -= 1
+                moved = True
+        if not moved: return 1e9, begun
+    return max(end.values()), begun
+
+
+def plan(ops, before):
+    n = len(ops)
+    known, need = [0] * n, []
+    for i in range(n):
+        keep, a = [], 0
+        for j in sorted(before[i], reverse=True):
+            if not (a >> j) & 1:
+                keep.append(j)
+                a |= known[j] | (1 << j)
+        known[i] = a
+        need.append(keep)
+    seqs = {q: [i for i in range(n) if ops[i][0] == q] for q in "vstgy"}
+    base = [walk(ops, need, seqs, m)[0] for m in MACHINES]
+    now, rng = 1.0, np.random.RandomState(4)
+    best = (now, seqs)
+    for turn in range(TRIES):
+        q = "vvvs"[rng.randint(4)]
+        row = list(seqs[q])
+        a, k = int(rng.randint(len(row))), 1 if rng.rand() < 0.6 else int(rng.randint(1, 8))
+        b = a + int(rng.randint(1, 40)) * (1 if rng.rand() < 0.5 else -1)
+        lim = now - 0.0006 * max(0.0, 1.0 - 1.2 * turn / TRIES) * math.log(rng.rand() + 1e-12)
+        run = row[a:a + k]
+        del row[a:a + k]
+        b = max(0, min(len(row), b))
+        mid = row[min(a, b):max(a, b)]
+        if b > a and any([j in run for i in mid for j in need[i]]): continue
+        if b < a and any([j in mid for i in run for j in need[i]]): continue
+        row[b:b] = run
+        new = dict(seqs)
+        new[q] = row
+        total = 0.0
+        for m, w in zip(MACHINES, base):
+            r = walk(ops, need, new, m)[0] / w
+            total += r / len(MACHINES)
+            if r > lim + 0.03: total += 9.0
+            if total > lim: break
+        if total <= lim:
+            now, seqs = total, new
+            if now < best[0]: best = (now, seqs)
+    begun = walk(ops, need, best[1], MACHINES[1])[1]
+    return [i for t, i in sorted([(begun[i], i) for i in range(n)])]

import math
import numpy as np
from concourse.mybir import dt, AluOpType as OP, ActivationFunctionType as AF

C, B = 320, 160
STEP = [1, 2, 4]
EW = 176
WD = C + EW
NE = [160, 162, 160]
F8, BF, F32, U16, U8, I32 = "float8_e4m3fn_x4", "bfloat16", "float32", "uint16", "uint8", "int32"
CYCLE = 0.00104
LW = 640
PB = 839

SCRATCH = {
    "oi": ("sbuf", [128, 20], I32), "mi": ("sbuf", [128, 20], I32),
    "x0": ("sbuf", [128, 4 * C], BF), "ut": ("sbuf", [128, 512], BF), "vt": ("sbuf", [128, 512], BF),
    "wq": ("sbuf", [128, 512], F8), "wp": ("sbuf", [128, 512], U8),
    "uq": ("sbuf", [128, 128], F8), "up": ("sbuf", [128, 128], U8),
    "uq16": ("sbuf", [128, 128], F8), "up16": ("sbuf", [128, 128], U8),
    "vq": ("sbuf", [128, 128], F8), "vp": ("sbuf", [128, 128], U8),
    "ect": ("sbuf", [128, 516], BF), "ones": ("sbuf", [128, 516], BF),
    "eq": ("sbuf", [128, 512], F8), "ep": ("sbuf", [128, 512], U8),
    "iota": ("sbuf", [128, C], BF), "cw": ("sbuf", [128, C], BF), "bw": ("sbuf", [128, B + 8], F32),
    "j16": ("sbuf", [128, C], BF), "mask": ("sbuf", [128, LW], BF), "hold": ("sbuf", [128, LW], BF),
    "pcol": ("sbuf", [128, 8], I32), "pcol2": ("sbuf", [128, 8], I32), "uli": ("sbuf", [128, 8], I32), "ulu": ("sbuf", [128, 8], U16),
    "kpat": ("sbuf", [128, 20], F32),
    "tb": ("sbuf", [128, 3000], F32), "ub": ("sbuf", [128, 1000], U16),
    "mrow": ("sbuf", [128, C], BF), "orow": ("sbuf", [128, C], BF), "prow": ("sbuf", [128, C], BF),
    "wf": ("sbuf", [128, 4 * WD], BF),
    "ah": ("sbuf", [128, 4 * C], BF), "af": ("sbuf", [128, 4 * C], BF),
    "et": ("sbuf", [128, 4 * 192], BF), "zt": ("sbuf", [128, 4 * C], BF), "xt": ("sbuf", [128, 4 * C], BF),
    "zq": ("sbuf", [128, C], F8), "zp": ("sbuf", [128, C], U8),
    "xq": ("sbuf", [128, C], F8), "xp": ("sbuf", [128, C], U8),
    "gs": ("sbuf", [128, 4 * C], F32), "sc": ("sbuf", [128, C], F32), "sb": ("sbuf", [128, B], F32),
    "ysb": ("sbuf", [128, C], F32), "romo": ("sbuf", [128, C], F32), "romm": ("sbuf", [128, C], F32),
}
for _t in range(3):
    for _n, _d in (("qe", F8), ("pe", U8), ("lq", F8), ("lp", U8)):
        SCRATCH[_n + str(_t)] = ("sbuf", [128, EW], _d)
    for _n, _w, _d in (("dl", 56, U16), ("tp", 352, BF), ("dr", 352, BF), ("er", 352, BF), ("bd", B, F32),
                       ("st", 80, I32), ("sh", 80, I32), ("cur", 80, I32), ("fg", 2 * LW, BF), ("fs", 2 * LW, BF)):
        SCRATCH[_n + str(_t)] = ("sbuf", [128, _w], _d)
for _k in range(10):
    SCRATCH["ra%d" % _k] = ("sbuf", [128, C], BF)
    SCRATCH["rs%d" % _k] = ("sbuf", [128, C], BF)
for _k in range(8):
    SCRATCH["ps%d" % _k] = ("psum", [128, 512], F32)
SEMAPHORES = ["vs", "ss", "ts", "gs"] + ["d%d" % k for k in range(16)] + ["arr%d" % k for k in range(3)] + ["loc%d" % k for k in range(3)]


def rank_program(g, core, T, topo):
    rank = T.rank_of(core)
    if rank is None:
        return
    queue = {"v": g.vector, "s": g.scalar, "t": g.tensor, "g": g, "y": g.sync}
    semof = {"v": "vs", "s": "ss", "t": "ts", "g": "gs"}
    count = {}
    clock = {q: {} for q in queue}
    snap = {}
    log = {}
    ndma = [0]

    def V(name, lo=0, hi=None, step=1):
        return (name, lo, SCRATCH[name][1][1] if hi is None else hi, step)

    def ap(v):
        return T[v[0]][:, v[1]:v[2]:v[3]] if v[3] != 1 else T[v[0]][:, v[1]:v[2]]

    def by(v):
        return ap(v).bitcast(dt.uint8)

    def ind(win, off):
        return ap(win).indirect(ap(off))

    def clash(a, b):
        if a[1] >= b[2] or b[1] >= a[2]: return False
        if a[3] == b[3] and a[3] > 1: return (a[1] - b[1]) % a[3] == 0
        return True

    def know(q, sem, val):
        if clock[q].get(sem, 0) >= val: return
        queue[q].wait_ge(T.sem[sem], val)
        for s, n in list(snap.get((sem, val), {}).items()) + [(sem, val)]:
            if clock[q].get(s, 0) < n: clock[q][s] = n

    def order(q, reads, writes):
        need = {}
        for vs, isw in ((reads, False), (writes, True)):
            for v in vs:
                psum = v[0][:2] == "ps"
                for (w, sem, val, oldw, oq) in log.get(v[0], ()):
                    if (isw or oldw or (psum and oq != q)) and (psum or clash(v, w)):
                        if need.get(sem, 0) < val: need[sem] = val
        for sem, val in sorted(need.items(), key=lambda k: -k[1]):
            know(q, sem, val)

    def note(q, sem, val, reads, writes):
        snap[(sem, val)] = dict(clock.get(q, {}))
        for vs, isw in ((reads, False), (writes, True)):
            for v in vs:
                old = log.setdefault(v[0], [])
                if isw:
                    old[:] = [r for r in old if not (v[3] == 1 and v[1] <= r[0][1] and r[0][2] <= v[2])]
                old.append((v, sem, val, isw, q))

    calls = []

    def put(q, issue, reads, writes, cost, late=0.0):
        calls.append((q, issue, reads, writes, cost, late))

    def run(q, fn, reads, writes, kind=""):
        def issue():
            order(q, reads, writes)
            s = semof[q]
            count[s] = count.get(s, 0) + 1
            fn().then_inc(T.sem[s], 1)
            note(q, s, count[s], reads, writes)
        o = writes[0]
        n = (o[2] - o[1] + o[3] - 1) // o[3]
        narrow = all(SCRATCH[v[0]][2] in (BF, U16) for v in reads + writes)
        psum = any(v[0][:2] == "ps" for v in reads)
        if kind == "ind": c = 0.055 + 1.56 * CYCLE * n
        elif kind == "scat": c = 3.5 * CYCLE * n
        elif kind == "q": c = 0.015 + 4 * 0.00028 * n
        elif q == "t": c = (n + 16) * CYCLE * 1.2
        elif q == "g": c = 0.17 + 2 * CYCLE * n
        elif q == "s": c = CYCLE * max(n, 64) + 0.1
        else: c = CYCLE * max(64, n * (2 if kind == "tt" and not psum else 0.5 if narrow else 1))
        put(q, issue, reads, writes, c)

    def dma(q, pairs, reads, writes):
        def issue():
            order(q, reads, writes)
            s = "d%d" % ndma[0]
            ndma[0] += 1
            for o, i in pairs:
                queue[q].dma_start(o, i).then_inc(T.sem[s], 16)
            count[s] = 16 * len(pairs)
            note(q, s, count[s], reads, writes)
        big = writes and SCRATCH[writes[0][0]][1][1] > 500
        put(q, issue, reads, writes, 0.07 * len(pairs), 4.0 if big else 2.2)

    def copy(out, a):
        run("v", lambda: g.vector.tensor_copy(ap(out), ap(a)), [a], [out])

    def tt(out, a, b, op):
        run("v", lambda: g.vector.tensor_tensor(ap(out), ap(a), ap(b), op), [a, b], [out], "tt")

    def ts(out, a, s1, op0, s2=None, op1=None):
        if op1 is None:
            run("v", lambda: g.vector.tensor_scalar(ap(out), ap(a), s1, None, op0), [a], [out])
        else:
            run("v", lambda: g.vector.tensor_scalar(ap(out), ap(a), s1, s2, op0, op1), [a], [out])

    def tsp(out, a, col, op):
        run("v", lambda: g.vector.tensor_scalar(ap(out), ap(a), ap(col), None, op), [a, col], [out])

    def tti(out, win, off, b, op):
        run("v", lambda: g.vector.tensor_tensor(ap(out), ind(win, off), ap(b), op), [win, off, b], [out], "ind")

    def tsi(out, win, off, s1, op0):
        run("v", lambda: g.vector.tensor_scalar(ap(out), ind(win, off), s1, None, op0), [win, off], [out], "ind")

    def fill(out, c):
        run("v", lambda: g.vector.memset(ap(out), c), [], [out])

    def act(out, a, scale=1.0):
        run("s", lambda: g.scalar.activation(ap(out), ap(a), AF.Copy, scale=scale), [a], [out])

    def acti(out, win, off, scale=1.0):
        run("s", lambda: g.scalar.activation(ap(out), ind(win, off), AF.Copy, scale=scale), [win, off], [out], "ind")

    def actb(out, win, off, bias):
        run("s", lambda: g.scalar.activation(ap(out), ind(win, off), AF.Identity, bias=bias), [win, off], [out], "ind")

    def quant(q, p, a):
        run("v", lambda: g.vector.quantize_mx(ap(q), ap(p), ap(a)), [a], [q, p], "q")

    def mm(out, l, lp, r, rp):
        run("t", lambda: g.tensor.matmul_mx(ap(out), ap(l), ap(lp), ap(r), ap(rp), True, True), [l, lp, r, rp], [out])

    def iota(out, pattern, base, cm):
        run("g", lambda: g.iota(ap(out), pattern, base, cm, allow_small_or_imprecise_dtypes=True), [], [out])

    ntb, nub, nrow = [0], [0], [0]

    def tmp(n):
        ntb[0] += n
        return V("tb", ntb[0] - n, ntb[0])

    def lst(n):
        nub[0] += n + n % 2
        return V("ub", nub[0] - n - n % 2, nub[0] - n % 2)

    def sub(v, lo, hi, step=1):
        if v[3] == 1: return (v[0], v[1] + lo, v[1] + hi, step)
        return (v[0], v[1] + lo * v[3], min(v[2], v[1] + (hi - 1) * v[3] + 1), v[3] * step)

    def tab(v, lo, hi):
        return (v[0], v[1] + 16 * lo + 15, v[1] + 16 * hi, 16)

    def scan(out, data):
        h = V("hold", 0, data[2] - data[1])
        run("v", lambda: g.vector.tensor_tensor_scan(ap(out), ap(h), ap(data), 0.0, OP.mult, OP.add), [h, data], [out])

    def lookup(raw, out, win, off):
        tti(raw, win, off, V("mask", 0, raw[2] - raw[1]), OP.mult)
        scan(out, raw)

    def look20(win, off):
        k = nrow[0]
        nrow[0] += 1
        lookup(V("ra%d" % k), V("rs%d" % k), win, off)
        return tab(V("rs%d" % k), 0, 20)

    def win0(name):
        return V(name, 16, 16 + C)

    def first_of(name, k):
        return V(name, 16 - k, 16 - k + C - 1, 2)

    def second_of(name, k):
        return V(name, 17 - k, 17 - k + C - 1, 2)

    def wf(b):
        return V("wf", b * WD, (b + 1) * WD)

    def wfF(b):
        return V("wf", b * WD, b * WD + C)

    def el(b):
        return (b, 4 * C - 3 + b, 4)

    def cols(name, b, n=128):
        return V(name, n * b, n * b + n)

    dma("y", [(T.oi[:], T.o[:]), (T.mi[:], T.m[:])], [], [V("oi"), V("mi")])
    dma("s", [(T.x0[:], T.x[:])], [], [V("x0")])
    dma("y", [(T.ut[:], T.u[:])], [], [V("ut")])
    dma("y", [(by(V("wq")), T.wc[:]), (T.wp[:], T.ws[:])], [], [V("wq"), V("wp")])
    dma("y", [(T.vt[:], T.v[:])], [], [V("vt")])

    iota(V("pcol"), [[0, 8]], 0, 1)
    iota(V("kpat"), [[32, 10], [1, 2]], 0, 0)
    iota(V("j16"), [[0, C // 16], [1, 16]], 0, 0)
    iota(V("iota"), [[1, C]], -B, 0)
    iota(V("uli"), [[16, 8]], 0, 0)
    fill(V("ones"), 1.0)
    run("g", lambda: g.affine_select(T.ect[:], T.ones[:], [[1, 516]], OP.is_equal, 0.0, -3, -4), [V("ones")], [V("ect")])
    iota(V("cw"), [[1024, C]], -1024 * B, 0)
    pm, pm2 = tmp(1), tmp(1)
    ts(V("pcol2"), V("pcol"), 15, OP.bitwise_and)
    copy(pm, V("pcol2", 0, 1))
    ts(pm2, pm, 2.0, OP.mult)
    K = [tmp(20), tmp(20)]
    tsp(K[0], V("kpat"), pm2, OP.add)
    ts(K[1], K[0], -1.0, OP.add)
    ku0, first = lst(20), tmp(10)
    copy(ku0, K[0])
    ts(first, sub(K[1], 0, 20, 2), 0.0, OP.is_lt)
    last, K2 = tmp(20), tmp(20)
    ts(last, K[1], 0.0, OP.is_lt, float(C), OP.mult)
    tt(K2, K[1], last, OP.add)
    for t in range(3):
        kA = sub(K[t % 2], 0, 20, 2)
        ts(V("dl%d" % t, 0, 6), sub(kA, 0, 6), 0.0, OP.max)
        ts(V("dl%d" % t, 26, 36), kA, 0.0, OP.max)
    tsp(V("mask", 0, C), V("j16"), pm, OP.is_equal)
    run("s", lambda: g.scalar.activation(ap(V("hold", 0, C)), T.j16[:], AF.Sign), [V("j16")], [V("hold", 0, C)])
    act(V("mask", C, LW), V("mask", 0, C))
    act(V("hold", C, LW), V("hold", 0, C))
    for v, z in ((V("bw", 0, B + 1), -1e29), (V("bw", B + 1, B + 8), 1e29)):
        run("s", lambda v=v, z=z: g.scalar.activation(ap(v), ap(V("j16", 0, v[2] - v[1])), AF.Identity, bias=z, scale=0.0), [V("j16")], [v])
    for v in [V("tp1", 328, 352), V("dr1", 328, 352)] + [V("wf", b * WD + C, (b + 1) * WD) for b in range(4)]:
        act(v, V("j16", 0, v[2] - v[1]), 0.0)
    onat, mu = lst(20), [lst(20) for k in range(4)]
    copy(onat, V("oi"))
    copy(mu[0], V("mi"))

    acti(V("orow"), V("iota"), onat)
    acti(V("mrow"), V("iota"), mu[0])
    run("v", lambda: g.vector.tensor_copy(ind(V("prow"), onat), ap(V("iota"))), [V("iota"), onat], [V("prow")], "scat")
    ot = look20(V("orow"), ku0)
    ou = lst(20)
    ts(ou, ot, float(B), OP.add)
    ts(V("cur0", 0, 20), ot, float(B), OP.add)
    for b in range(4):
        quant(cols("eq", b), cols("ep", b), V("ect", 3 - b, 515 - b))
    quant(V("xq"), V("xp"), V("x0"))
    xt0 = look20(V("mrow"), ou)
    xu = lst(20)
    ts(xu, xt0, float(B), OP.add)
    quant(V("uq"), V("up"), V("ut"))
    copy(V("ulu"), V("uli"))
    run("s", lambda: g.scalar.activation(T.up16[:], T.up[:].indirect(T.ulu[:]), AF.Copy), [V("up"), V("ulu")], [V("up16")], "ind")
    run("v", lambda: g.vector.tensor_copy(T.uq16[:].bitcast(dt.uint32), T.uq[:].bitcast(dt.uint32).indirect(T.ulu[:])), [V("uq"), V("ulu")], [V("uq16")], "ind")
    Mt0 = look20(V("prow"), xu)
    M0, x1 = tmp(20), tmp(20)
    ts(M0, Mt0, float(B), OP.add)

    def sides(y, M, o, k):
        d, b2 = tmp(20), tmp(20)
        tt(d, M, (K[0], K2)[k], OP.is_gt)
        ts(b2, o, float(B), OP.is_lt, 2.0, OP.mult)
        tt(y, d, b2, OP.add)

    def static(t, M):
        k = t % 2
        cur = V("cur%d" % t)
        o = sub(cur, 0, 20)
        oA, oB = sub(cur, 0, 20, 2), sub(cur, 1, 20, 2)
        y = sub(cur, 40, 60)
        if M is None: M = sub(cur, 60, 80)
        else: sides(y, M, o, 0)
        MA, MB = sub(M, 0, 20, 2), sub(M, 1, 20, 2)
        eq, gt, S, do, bi, biu = tmp(10), tmp(10), tmp(10), tmp(10), tmp(20), lst(20)
        ix, ixu = sub(bi, 10, 20), sub(biu, 10, 20)
        if k:
            bl = tmp(10)
            tt(bl, MA, sub(K[k], 1, 20, 2), OP.is_equal)
            tt(sub(bi, 0, 10), bl, first, OP.max)
        else:
            tt(sub(bi, 0, 10), MA, sub(K[k], 1, 20, 2), OP.is_equal)
        tt(eq, sub(y, 0, 20, 2), sub(y, 1, 20, 2), OP.is_equal)
        tt(gt, MA, MB, OP.is_gt)
        tt(S, eq, gt, OP.mult)
        tt(do, oB, oA, OP.subtract)
        tt(ix, do, S, OP.mult)
        ts(biu, bi, float(B), OP.add)
        acti(V("bd%d" % t), V("bw"), sub(biu, 0, 10))
        acti(first_of("dr%d" % t, k), V("cw"), ixu)
        acti(second_of("dr%d" % t, k), V("cw"), ixu)
        return dict(t=t, do=do, S=S, M=M, oA=oA, oB=oB)

    def static2(r):
        copy(V("dl%d" % r["t"], 6, 26), r["M"])
        r["oAu"], r["oBu"] = lst(10), lst(10)
        copy(r["oBu"], r["oB"])
        copy(r["oAu"], r["oA"])
        r["D"] = look20(win0("dr%d" % r["t"]), V("dl%d" % r["t"], 6, 26))

    def products(t):
        mm(V("ps4", 0, C), V("uq16"), V("up16"), V("xq"), V("xp"))
        for b in range(4):
            mm(V("ps%d" % b, 0, C), cols("eq", b), cols("ep", b), V("xq"), V("xp"))
        act(V("sc"), V("ps4", 0, C))
        for b in range(4):
            act(wfF(b), V("ps%d" % b, 0, C), 0.5)

    fill(V("cw", B, B + 1), 1.0)
    r = static(0, M0)
    ts(x1, xt0, 1024.0, OP.mult, 1024.0 * B, OP.add)
    tt(V("cur0", 20, 40), x1, M0, OP.add)
    products(0)
    static2(r)
    P = None
    for t in range(3):
        k = t % 2
        nl = 5 + k
        nu = 10 - nl
        dl, tp, er = "dl%d" % t, "tp%d" % t, "er%d" % t
        cur, st = V("cur%d" % t), V("st%d" % t)
        val = sub(cur, 20, 40)
        D, S, do = r["D"], r["S"], r["do"]
        tti(V("sb"), V("sc"), r["oBu"], V("bd%d" % t), OP.max)
        tti(first_of(tp, k), V("sc"), r["oAu"], V("sb"), OP.is_gt)
        ts(second_of(tp, k), first_of(tp, k), -1.0, OP.mult)
        fg, fs = "fg%d" % t, "fs%d" % t
        eu = lst(20)

        def renew(tc, tM, c0, c1):
            n = c1 - c0
            d1, alt, rr, dd, d2 = tmp(2 * n), tmp(2 * n), tmp(n), tmp(n), tmp(n)
            tt(d1, tM, sub(D, 2 * c0, 2 * c1), OP.mult)
            tt(rr, tc, sub(S, c0, c1), OP.is_gt)
            tt(alt, d1, sub(val, 2 * c0, 2 * c1), OP.add)
            aA, aB = sub(alt, 0, 2 * n, 2), sub(alt, 1, 2 * n, 2)
            tt(dd, aB, aA, OP.subtract)
            tt(d2, dd, rr, OP.mult)
            eA, eB = sub(st, 20 + 2 * c0, 20 + 2 * c1, 2), sub(st, 21 + 2 * c0, 20 + 2 * c1, 2)
            tt(eA, aA, d2, OP.add)
            tt(eB, aB, d2, OP.subtract)
            ts(sub(eu, c0, c1), eA, 1.0 / 1024, OP.mult)
            ts(sub(eu, 10 + c0, 10 + c1), eB, 1.0 / 1024, OP.mult)

        wl = 16 * (6 + 2 * nl)
        fl = V(fs, 0, wl)
        lookup(V(fg, 0, wl), fl, win0(tp), V(dl, 0, 6 + 2 * nl))
        renew(tab(fl, 0, nl), tab(fl, 6, 6 + 2 * nl), 0, nl)
        for b in range(4):
            acti(V("et", b, 128 * nl - 7 + b, 8), wfF(b), sub(eu, 0, nl), 2.0)
            tsi(V("et", 4 + b, 128 * nl - 3 + b, 8), wfF(b), sub(eu, 10, 10 + nl), 2.0, OP.mult)
        ne = NE[t]
        qe, pe, lq, lp = [V(s + str(t), 0, ne) for s in ("qe", "pe", "lq", "lp")]
        quant(qe, pe, V("et", 0, 4 * ne))
        dst = T.cores[rank ^ STEP[t]]
        rid, pid = topo.addr(dst)[:2]
        arr, loc, full = "arr%d" % t, "loc%d" % t, 2 * len(topo.engines(core, dst))

        def send(qe=qe, pe=pe, lq=lq, lp=lp, pid=pid, rid=rid, arr=arr, loc=loc, full=full, mask=topo.mask(core, dst)):
            order("g", [qe, pe], [])
            g.remote_dma(by(lq), by(qe), T.sem[arr], T.sem[loc], pid, rid, mask)
            g.remote_dma(ap(lp), ap(pe), T.sem[arr], T.sem[loc], pid, rid, mask)
            count[arr] = count[loc] = full
            note("g", loc, full, [qe, pe], [])
            log[lq[0]] = [(lq, arr, full, True, "r")]
            log[lp[0]] = [(lp, arr, full, True, "r")]

        put("g", send, [qe, pe], [lq, lp], 1.0, 2.2)
        for b in range(4):
            acti(cols("ah", b, C), wfF(b), mu[t])
        if t == 0:
            tt(V("ra8"), V("prow"), V("mask", 0, C), OP.mult)
            scan(V("rs8"), V("ra8"))
            p0 = tab(V("rs8"), 0, 20)
            ts(V("dl0", 36, 56), p0, float(B), OP.add)
            P = tmp(20)
            ts(P, p0, float(B - PB), OP.add)
        wu, lu = 16 * (2 * nu + 10), 6 + 2 * nl
        fv = V(fs, LW - C, LW - C + wu)
        lookup(V(fg, LW - C, LW - C + wu), fv, win0(tp), V(dl, lu, lu + 2 * nu + 10))
        tc = tab(fv, 2 * nu, 2 * nu + 10)
        renew(sub(tc, nl, 10), tab(fv, 0, 2 * nu), nl, 10)
        fu = V(fs, LW, LW + C)
        lookup(V(fg, LW, LW + C), fu, win0(tp), V(dl, 36, 56))
        acti(first_of(er, k), V("iota"), sub(eu, 0, 10))
        acti(second_of(er, k), V("iota"), sub(eu, 10, 20))
        if k: act(V(er, 16 + C - 1, 16 + C), V(er, 15, 16))
        pn, pf, pz, pu = tmp(20), tmp(20), tmp(20), lst(20) if t == 2 else V("dl%d" % (t + 1), 36, 56)
        tt(pn, P, tab(fu, 0, 20), OP.add)
        P = pn
        ts(pu, pn, float(PB), OP.add)
        t1 = tmp(10)
        tt(t1, tc, do, OP.mult)
        tt(sub(st, 0, 20, 2), sub(cur, 0, 20, 2), t1, OP.add)
        tt(sub(st, 1, 20, 2), sub(cur, 1, 20, 2), t1, OP.subtract)
        ts(pf, pn, float(B - PB), OP.is_lt, 1000.0, OP.mult)
        tt(pz, pf, pn, OP.add)
        if t == 2:
            ofu = lst(20)
            copy(sub(ofu, 0, 10), sub(st, 0, 20, 2))
            copy(sub(ofu, 10, 20), sub(st, 1, 20, 2))
        mn = look20(win0(er), pu)
        vm, vl = tmp(20), lst(20)
        tt(vm, pz, mn, OP.max)
        ts(vl, vm, float(B), OP.add)
        if t < 2:
            ts(sub(st, 60, 80), sub(st, 20, 40), 1023, OP.bitwise_and)
            sides(sub(st, 40, 60), sub(st, 60, 80), sub(st, 0, 20), k)
            s, h = T["st%d" % t], T["sh%d" % t]
            pairs = []
            if t == 0:
                for q in range(0, 128, 16):
                    pairs.append((h[q + 1:q + 16, :], s[q:q + 15, :]))
                for z in (0, 20, 40, 60):
                    pairs.append((h[0:128:16, z + 2:z + 20], s[15:128:16, z:z + 18]))
                    pairs.append((h[0:128:16, z:z + 2], s[15:128:16, z + 18:z + 20]))
            else:
                for q in range(0, 128, 16):
                    pairs.append((h[q:q + 15, :], s[q + 1:q + 16, :]))
                for z in (0, 20, 40, 60):
                    pairs.append((h[15:128:16, z:z + 18], s[0:128:16, z + 2:z + 20]))
                    pairs.append((h[15:128:16, z + 18:z + 20], s[0:128:16, z:z + 2]))
            dma("y", pairs, [st], [V("sh%d" % t)])
        for b in range(4):
            mm(V("ps%d" % b, 0, ne), cols("eq", b), cols("ep", b), lq, lp)
            act(V("wf", b * WD + C + 1 - k, b * WD + C + 1 - k + ne), V("ps%d" % b, 0, ne), 0.5)
        for b in range(4):
            tti(V("zt", *el(b)), wf(b), vl, cols("ah", b, C), OP.add)
        act(V("af"), V("ah"), 2.0)
        quant(V("zq"), V("zp"), V("zt"))
        ts(mu[t + 1], mn, float(B), OP.add)
        if t == 2:
            actb(V("romo", 0, C - 1, 2), V("iota"), sub(ofu, 0, 10), float(B))
            actb(V("romo", 1, C, 2), V("iota"), sub(ofu, 10, 20), float(B))
        for b in range(4):
            mm(V("ps%d" % (4 + b), 0, C), cols("wq", b), cols("wp", b), V("zq"), V("zp"))
            act(cols("gs", b, C), V("ps%d" % (4 + b), 0, C), 0.0078125)
        if t < 2:
            n, h = "cur%d" % (t + 1), "sh%d" % t
            if t == 0:
                copy(V(n, 0, 79, 2), V(h, 1, 80, 2))
                copy(V(n, 1, 80, 2), V("st0", 0, 79, 2))
            else:
                copy(V(n, 0, 79, 2), V("st1", 1, 80, 2))
                copy(V(n, 1, 80, 2), V(h, 0, 79, 2))
            r = static(t + 1, None)
        else:
            quant(V("vq"), V("vp"), V("vt"))
        for b in range(4):
            tti(V("xt", *el(b)), cols("gs", b, C), mu[t + 1], cols("af", b, C), OP.add)
        quant(V("xq"), V("xp"), V("xt"))
        if t < 2:
            products(t + 1)
            static2(r)
    for z in range(2):
        mm(V("ps%d" % (4 + z), 0, B), V("vq"), V("vp"), V("xq", B * z, B * z + B), V("xp", B * z, B * z + B))
    dma("y", [(T.oc[:], by(V("xq")))] + [(T.osc[4 * q:4 * q + 4, :], T.xp[32 * q:32 * q + 4, :]) for q in range(4)], [V("xq"), V("xp")], [])
    act(V("ysb", 0, B), V("ps4", 0, B))
    copy(V("ysb", B, C), V("ps5", 0, B))
    dma("s", [(T.y[:, 0:B], T.ysb[:, 0:B])], [V("ysb", 0, B)], [])
    dma("s", [(T.y[:, B:C], T.ysb[:, B:C])], [V("ysb", B, C)], [])
    actb(V("romm"), V("iota"), mu[3], float(B))
    dma("y", [(T.om[:, 0:C], T.romo[0:128:16, :]), (T.om[:, C:2 * C], T.romm[0:128:16, :])], [V("romo"), V("romm")], [])
    if "plan" not in PLAN:
        seen, before = {}, []
        for i, (q, issue, reads, writes, cost, late) in enumerate(calls):
            p = set()
            for vs, isw in ((reads, False), (writes, True)):
                for v in vs:
                    psum = v[0][:2] == "ps"
                    for w, j, oldw in seen.get(v[0], ()):
                        if (isw or oldw or (psum and calls[j][0] != q)) and (psum or clash(v, w)): p.add(j)
            for vs, isw in ((reads, False), (writes, True)):
                for v in vs: seen.setdefault(v[0], []).append((v, i, isw))
            before.append(sorted(p))
        PLAN["plan"] = plan([(c[0], c[4], c[5]) for c in calls], before)
    for i in PLAN["plan"]:
        calls[i][1]()
    for sem, n in count.items():
        know("g", sem, n)


PLAN = {}
MACHINES = [(1.0, 0.06, 0.0, 0.0), (1.1, 0.1, 0.06, 0.5), (1.2, 0.15, 0.1, 1.0), (0.9, 0.08, 0.05, 2.0)]
TRIES = 170000


def walk(ops, before, seqs, m):
    fac, wake, own, more = m
    end, at, free = {}, {q: 0 for q in seqs}, {q: 0.0 for q in seqs}
    begun = {}
    left = len(ops)
    while left:
        moved = False
        for q, seq in seqs.items():
            while at[q] < len(seq):
                i = seq[at[q]]
                t, late = free[q], False
                ok = True
                for j in before[i]:
                    if j not in end:
                        ok = False
                        break
                if not ok: break
                for j in before[i]:
                    e = end[j] + (own if ops[j][0] == q and end[j] >= free[q] - 1e-9 else wake if ops[j][0] != q and end[j] > free[q] else 0.0)
                    if e > t: t = e
                begun[i] = t
                free[q] = t + ops[i][1] * (fac if q in "vs" else 1.0)
                end[i] = free[q] + (ops[i][2] + more if ops[i][2] else 0.0)
                at[q] += 1
                left -= 1
                moved = True
        if not moved: return 1e9, begun
    return max(end.values()), begun


def plan(ops, before):
    n = len(ops)
    known, need = [0] * n, []
    for i in range(n):
        keep, a = [], 0
        for j in sorted(before[i], reverse=True):
            if not (a >> j) & 1:
                keep.append(j)
                a |= known[j] | (1 << j)
        known[i] = a
        need.append(keep)
    seqs = {q: [i for i in range(n) if ops[i][0] == q] for q in "vstgy"}
    base = [walk(ops, need, seqs, m)[0] for m in MACHINES]
    now, rng = 1.0, np.random.RandomState(4)
    best = (now, seqs)
    for turn in range(TRIES):
        q = "vvvs"[rng.randint(4)]
        row = list(seqs[q])
        a, k = int(rng.randint(len(row))), 1 if rng.rand() < 0.6 else int(rng.randint(1, 8))
        b = a + int(rng.randint(1, 40)) * (1 if rng.rand() < 0.5 else -1)
        lim = now - 0.0006 * max(0.0, 1.0 - 1.2 * turn / TRIES) * math.log(rng.rand() + 1e-12)
        run = row[a:a + k]
        del row[a:a + k]
        b = max(0, min(len(row), b))
        mid = row[min(a, b):max(a, b)]
        if b > a and any([j in run for i in mid for j in need[i]]): continue
        if b < a and any([j in mid for i in run for j in need[i]]): continue
        row[b:b] = run
        new = dict(seqs)
        new[q] = row
        total = 0.0
        for m, w in zip(MACHINES, base):
            r = walk(ops, need, new, m)[0] / w
            total += r / len(MACHINES)
            if r > lim + 0.03: total += 9.0
            if total > lim: break
        if total <= lim:
            now, seqs = total, new
            if now < best[0]: best = (now, seqs)
    begun = walk(ops, need, best[1], MACHINES[1])[1]
    return [i for t, i in sorted([(begun[i], i) for i in range(n)])]
